import numpy as np
import ml_dtypes


def mxq(x, axis, fmt="e4m3"):
    dtype, down = {"e4m3": (ml_dtypes.float8_e4m3fn, 7), "e5m2": (ml_dtypes.float8_e5m2, 14)}[fmt]
    v = np.moveaxis(np.asarray(x, np.float32).astype(ml_dtypes.bfloat16).astype(np.float64), axis, -1)
    blocks = v.reshape(v.shape[:-1] + (-1, 32))
    amax = np.abs(blocks).max(-1, keepdims=True)
    byte = np.maximum(np.where(amax > 0, np.frexp(amax)[1] - 1 + 127, 0) - down, 1)
    scale = np.exp2(byte - 127.0)
    codes = (blocks / scale).astype(np.float32).astype(dtype).astype(np.float64)
    return np.moveaxis((codes * scale).reshape(v.shape), -1, axis)


WIDE = False


def mx_kscale(k):
    if not WIDE:
        return np.ones(k)
    levels = np.array([10, -10, 5, -5, 0])
    if k % 512:
        return np.exp2(np.random.permutation(np.resize(levels, k // 32))).repeat(32)
    a = np.empty((k // 512, 16))
    for p in range(k // 512):
        a[p, :8] = np.random.permutation(np.resize(levels, 8))
        for g in range(8):
            far = levels[np.abs(levels - a[p, g]) >= 10]
            a[p, g + 8] = far[np.random.randint(len(far))]
    return np.exp2(a.ravel()).repeat(32)


def f64(x):
    return np.asarray(x).astype(np.float64)


def striped(idx):
    return np.tile(idx.reshape(-1, 16).T, (8, 1)).astype(np.uint16)


def unstriped(offs):
    return offs[:16].T.reshape(-1).astype(np.int64)


E2M1 = np.array([0.0, 0.5, 1.0, 1.5, 2.0, 3.0, 4.0, 6.0, -0.0, -0.5, -1.0, -1.5, -2.0, -3.0, -4.0, -6.0])


def pack_fp4(w):
    k, n = w.shape
    w = f64(np.asarray(w, np.float32).astype(ml_dtypes.bfloat16)).reshape(k // 32, 32, n)
    amax = np.abs(w).max(1)
    mant, ex = np.frexp(amax / 6.0)
    byte = np.clip(np.where(amax > 0, np.where(mant > 0.5, ex, ex - 1) + 127, 1), 1, 254)
    scaled = (w * np.exp2(127.0 - byte)[:, None, :]).reshape(k, n).astype(np.float32)
    c = np.ascontiguousarray(scaled.reshape(k // 512, 128, 4, n).transpose(0, 1, 3, 2)).astype(ml_dtypes.float4_e2m1fn).view(np.uint8) & 0xF
    words = (c[..., 0::2] | (c[..., 1::2] << 4)).reshape(k // 512, 128, 2 * n)
    return np.ascontiguousarray(words), np.ascontiguousarray(byte.astype(np.uint8).reshape(k // 512, 16, n))


def unpack_fp4(words, scales):
    g, _, n = scales.shape
    words = np.ascontiguousarray(words).reshape(g, 128, n, 2)
    nib = np.empty((g, 128, n, 4), np.uint8)
    nib[..., 0::2] = words & 0xF
    nib[..., 1::2] = words >> 4
    vals = E2M1[nib] * np.repeat(np.exp2(scales.astype(np.float64) - 127.0), 8, axis=1)[..., None]
    return vals.transpose(0, 1, 3, 2).reshape(g * 512, n)


def relu(v):
    return np.maximum(v, 0.0)


K, T, S, D, V, H, N, U = 1024, 2048, 1024, 2, 512, 512, 256, 256
P = 2 ** 7


def setup_inputs():
    n = np.random.standard_normal
    s = mx_kscale(K)[:, None]
    u = mx_kscale(H)
    packed_w2 = pack_fp4(n((H, N)) / np.sqrt(H) / u[:, None])
    return {
        "xT": (n((K, T)) * s).astype(np.float32),
        "w1": (n((K, H)) / np.sqrt(K) / s * u).astype(np.float32),
        "w2_words": packed_w2[0],
        "w2_scales": packed_w2[1],
        "gate": (np.tile(np.random.uniform(0.2, 1.0, (D, 1, V)) / np.sqrt(D), (1, P, 1))).astype(np.float32),
        "gate2": (np.tile(np.random.uniform(0.2, 1.0, (D, 1, U)) / np.sqrt(D), (1, P, 1))).astype(np.float32),
        "offs": striped(np.random.permutation(T)[:S]),
        "pos1": striped(np.random.permutation(S)[:V]),
        "pos2": striped(np.random.permutation(S)[:V]),
        "nxt1": striped(np.random.permutation(V)[:U]),
        "nxt2": striped(np.random.permutation(V)[:U]),
    }


def reference(xT, w1, w2_words, w2_scales, gate, gate2, offs, pos1, pos2, nxt1, nxt2):
    xq = mxq(f64(xT)[:, unstriped(offs)], 0, "e4m3")
    h = relu(mxq(f64(w1), 0, "e4m3").T @ xq)
    z = h[:, unstriped(pos1)] * f64(gate)[0, :1] + h[:, unstriped(pos2)] * f64(gate)[1, :1]
    g = relu(unpack_fp4(w2_words, w2_scales).T @ mxq(z, 0, "e4m3"))
    return g[:, unstriped(nxt1)] * f64(gate2)[0, :1] + g[:, unstriped(nxt2)] * f64(gate2)[1, :1]

@@ -1,0 +1,200 @@
+from contextlib import ExitStack
+
+import concourse.mybir as mybir
+
+K, T, S, V, H, N, U = 1024, 2048, 1024, 512, 512, 256, 256
+FLOPS = 2 * K * H * S + 2 * H * N * V
+
+F32 = mybir.dt.float32
+BF16 = mybir.dt.bfloat16
+I32 = mybir.dt.int32
+U32 = mybir.dt.uint32
+U16 = mybir.dt.uint16
+U8 = mybir.dt.uint8
+FP8X4 = mybir.dt.float8_e4m3fn_x4
+FP4X4 = mybir.dt.float4_e2m1fn_x4
+COPY = mybir.ActivationFunctionType.Copy
+RELU = mybir.ActivationFunctionType.Relu
+MULT = mybir.AluOpType.mult
+ADD = mybir.AluOpType.add
+
+P = 128
+PACK = 4
+K_PASS = P * PACK
+PASSES = K // K_PASS
+BANK = 512
+STRIPE = 16
+
+X_CHUNKS = [
+    [(512, 320), (512, 320), (512, 320), (512, 320)],
+    [(512, 320), (512, 320), (512, 320), (256, 96), (256, 96)],
+]
+W_PIECES = [(0, 0, 256), (0, 256, 256), (1, 0, 256), (1, 256, 256)]
+Z_PIECES = [(0, 256), (256, 256)]
+
+
+def tile_picked_hop2_relu_e_kernel(
+    tc, xT, w1, w2_words, w2_scales, gate, gate2, offs, pos1, pos2, nxt1, nxt2, out
+):
+    nc = tc.nc
+    with ExitStack() as ctx:
+        lists = ctx.enter_context(tc.tile_pool(name="lists", bufs=1))
+        keep = ctx.enter_context(tc.tile_pool(name="keep", bufs=1))
+        psum = ctx.enter_context(tc.psum_pool(name="psum", bufs=1))
+
+        def load_list(src, name):
+            tile = lists.tile(list(src.shape), U16, name=name)
+            nc.sync.dma_start(tile[:], src)
+            return tile
+
+        x_scales = keep.tile([P, T], U8, name="x_scales", tag="x_scales", align_bytes=64)
+        nc.gpsimd.memset(x_scales[:], 0)
+        w2_plane = keep.tile([P, N], U8, name="w2_plane", align_bytes=64)
+        nc.gpsimd.memset(w2_plane[:], 0)
+
+        x_raw = []
+        offs_t = None
+        for g in range(PASSES):
+            c0 = 0
+            rows = xT[g * K_PASS : (g + 1) * K_PASS, :].rearrange("(p j) c -> p j c", j=PACK)
+            for n, (width, share) in enumerate(X_CHUNKS[g]):
+                raw = keep.tile([P, PACK, width], F32, name=f"x_raw{g}_{n}")
+                nc.sync.dma_start(raw[:], rows[:, :, c0 : c0 + width])
+                x_raw.append((g, c0, width, share, raw))
+                c0 += width
+            if g == 0:
+                offs_t = load_list(offs, "offs_t")
+        w_raw = []
+        for n, (g, c0, width) in enumerate(W_PIECES):
+            rows = w1[g * K_PASS : (g + 1) * K_PASS, :].rearrange("(p j) c -> p j c", j=PACK)
+            raw = keep.tile([P, PACK, width], F32, name=f"w_raw{n}")
+            nc.sync.dma_start(raw[:], rows[:, :, c0 : c0 + width])
+            w_raw.append(raw)
+        pos_t, gate_t = [], []
+        for d, src in enumerate((pos1, pos2)):
+            pos_t.append(load_list(src, f"pos_t{d}"))
+            tile = keep.tile([P, V], F32, name=f"gate_t{d}")
+            nc.sync.dma_start(tile[:], gate[d])
+            gate_t.append(tile)
+        w2_codes = keep.tile([P, 2 * N], U8, name="w2_codes", align_bytes=64)
+        nc.sync.dma_start(w2_codes[:], w2_words[0])
+        for q in range(4):
+            nc.sync.dma_start(
+                w2_plane[32 * q : 32 * q + 4, :].bitcast(I32), w2_scales[0, 4 * q : 4 * q + 4, :].bitcast(I32)
+            )
+        nxt_t, gate2_t = [], []
+        for d, src in enumerate((nxt1, nxt2)):
+            nxt_t.append(load_list(src, f"nxt_t{d}"))
+            tile = keep.tile([P, U], F32, name=f"gate2_t{d}")
+            nc.sync.dma_start(tile[:], gate2[d])
+            gate2_t.append(tile)
+
+        x_words = [keep.tile([P, T], U32, name=f"x_words{g}", align_bytes=64) for g in range(PASSES)]
+        halves = S // BANK
+        cols = BANK // STRIPE
+        picked0 = keep.tile([P, S], U32, name="picked0", align_bytes=64)
+
+        def quantise_chunk(n):
+            g, c0, width, share, raw = x_raw[n]
+            nc.vector.quantize_mx(
+                out=x_words[g][:, c0 : c0 + width].bitcast(FP8X4),
+                scales=x_scales[4 * g : P, c0 : c0 + width],
+                in_=x_bf[n][:].rearrange("p c j -> p (c j)"),
+            )
+
+        x_bf = []
+        first_of_pass1 = len(X_CHUNKS[0])
+        for n, (g, c0, width, share, raw) in enumerate(x_raw):
+            grouped = keep.tile([P, width, PACK], BF16, name=f"x_bf{n}", align_bytes=64)
+            x_bf.append(grouped)
+            dst = grouped[:].rearrange("p (c i) j -> p c j i", i=4)
+            src = raw[:].rearrange("p j (c i) -> p c j i", i=4)
+            nc.scalar.activation(dst[:, : share // 4], src[:, : share // 4], COPY)
+            nc.vector.tensor_copy(dst[:, share // 4 :], src[:, share // 4 :])
+            quantise_chunk(n)
+            if n == first_of_pass1:
+                nc.vector.tensor_copy(picked0[:], x_words[0][:].indirect(offs_t[:]))
+
+        w_bf = [keep.tile([P, PACK, P, PACK], BF16, name=f"w_bf{g}", tag=f"w_bf{g}", align_bytes=64) for g in range(PASSES)]
+        w_words = [keep.tile([P, H], U32, name=f"w_words{g}", align_bytes=64) for g in range(PASSES)]
+        w_scales = [keep.tile([P, H], U8, name=f"w_scales{g}", align_bytes=64) for g in range(PASSES)]
+
+        for n, (g, c0, width) in enumerate(W_PIECES):
+            dst = w_bf[g][:, :, c0 // 4 : (c0 + width) // 4, :].rearrange("p t m j -> p m t j")
+            nc.scalar.activation(dst, w_raw[n][:].rearrange("p j (m t) -> p m t j", t=PACK), COPY)
+
+        picked_scales, picked1 = [], []
+
+        def gather_half(b, tag, word_tag):
+            part = offs_t[:, b * cols : (b + 1) * cols]
+            tile = keep.tile([P, BANK], U8, name=f"picked_scales{b}", tag=tag, align_bytes=64)
+            picked_scales.append(tile)
+            nc.vector.tensor_copy(tile[:], x_scales[:].indirect(part))
+            words = keep.tile([P, BANK], U32, name=f"picked1_{b}", tag=word_tag, align_bytes=64)
+            picked1.append(words)
+            nc.vector.tensor_copy(words[:], x_words[1][:].indirect(part))
+
+        gather_half(0, "picked_scales0", "picked1_0")
+        nc.vector.quantize_mx(
+            out=w_words[0][:].bitcast(FP8X4), scales=w_scales[0][:], in_=w_bf[0][:].rearrange("p t m j -> p (t m j)")
+        )
+        gather_half(1, "w_bf0", "x_scales")
+        for t in range(PACK):
+            nc.vector.quantize_mx(
+                out=w_words[1][:, t * P : (t + 1) * P].bitcast(FP8X4),
+                scales=w_scales[1][:, t * P : (t + 1) * P],
+                in_=w_bf[1][:, t].rearrange("p m j -> p (m j)"),
+            )
+
+        terms = [keep.tile([P, PACK, V], F32, name=f"terms{d}") for d in range(2)]
+        for t in range(PACK):
+            h = keep.tile([P, S], F32, name=f"h{t}")
+            banks = [psum.tile([P, BANK], F32, name=f"bank{2 * t + b}", tag=f"bank{(2 * t + b) % 4}") for b in range(halves)]
+            for g in range(PASSES):
+                for b in range(halves):
+                    moving = picked0[:, b * BANK : (b + 1) * BANK] if g == 0 else picked1[b][:]
+                    nc.tensor.matmul_mx(
+                        out=banks[b][:],
+                        lhsT=w_words[g][:, t * P : (t + 1) * P].bitcast(FP8X4),
+                        lhsT_scale=w_scales[g][:, t * P : (t + 1) * P],
+                        rhs=moving.bitcast(FP8X4),
+                        rhs_scale=picked_scales[b][4 * g : P, :],
+                        start=(g == 0),
+                        stop=(g == PASSES - 1),
+                    )
+            for b in range(halves):
+                nc.scalar.activation(h[:, b * BANK : (b + 1) * BANK], banks[b][:], RELU)
+            for d in range(2):
+                nc.vector.tensor_tensor(terms[d][:, t, :], h[:].indirect(pos_t[d][:]), gate_t[d][:], MULT)
+
+        g_rows = [keep.tile([P, V], F32, name=f"g_rows{m}") for m in range(N // P)]
+        z_bf = [keep.tile([P, w, PACK], BF16, name=f"z_bf{n}", align_bytes=64) for n, (v0, w) in enumerate(Z_PIECES)]
+        for n, (v0, width) in enumerate(Z_PIECES):
+            views = [terms[d][:, :, v0 : v0 + width].rearrange("p t (c i) -> p c t i", i=4) for d in range(2)]
+            nc.vector.tensor_tensor(z_bf[n][:].rearrange("p (c i) t -> p c t i", i=4), views[0], views[1], ADD)
+        for n, (v0, width) in enumerate(Z_PIECES):
+            z_words = keep.tile([P, width], U32, name=f"z_words{n}", align_bytes=64)
+            z_scales = keep.tile([P, width], U8, name=f"z_scales{n}", align_bytes=64)
+            nc.vector.quantize_mx(
+                out=z_words[:].bitcast(FP8X4), scales=z_scales[:], in_=z_bf[n][:].rearrange("p v t -> p (v t)")
+            )
+            for m in range(N // P):
+                bank = psum.tile([P, BANK], F32, name=f"g_bank{2 * n + m}", tag=f"bank{4 + 2 * n + m}")
+                nc.tensor.matmul_mx(
+                    out=bank[:, :width],
+                    lhsT=w2_codes[:, 2 * P * m : 2 * P * (m + 1)].bitcast(FP4X4),
+                    lhsT_scale=w2_plane[:, P * m : P * (m + 1)],
+                    rhs=z_words[:].bitcast(FP8X4),
+                    rhs_scale=z_scales[:],
+                    start=True,
+                    stop=True,
+                )
+                nc.scalar.activation(g_rows[m][:, v0 : v0 + width], bank[:, :width], RELU)
+
+        for m in range(N // P):
+            parts = [keep.tile([P, U], F32, name=f"parts{m}_{d}") for d in range(2)]
+            for d in range(2):
+                nc.vector.tensor_tensor(parts[d][:], g_rows[m][:].indirect(nxt_t[d][:]), gate2_t[d][:], MULT)
+            result = keep.tile([P, U], F32, name=f"result{m}")
+            nc.vector.tensor_tensor(result[:], parts[0][:], parts[1][:], ADD)
+            nc.sync.dma_start(out[m * P : (m + 1) * P, :], result[:])

@@ -26,10 +26,10 @@ BANK = 512
 STRIPE = 16
 
 X_CHUNKS = [
-    [(512, 320), (512, 320), (512, 320), (512, 320)],
-    [(512, 320), (512, 320), (512, 320), (256, 96), (256, 96)],
+    [(512, 256), (512, 256), (512, 256), (512, 160)],
+    [(512, 448), (512, 256), (512, 176), (256, 160), (128, 128), (128, 0)],
 ]
-W_PIECES = [(0, 0, 256), (0, 256, 256), (1, 0, 256), (1, 256, 256)]
+W_HALF = H // 2
 Z_PIECES = [(0, 256), (256, 256)]
 
 
@@ -65,10 +65,11 @@ def tile_picked_hop2_relu_e_kernel(
             if g == 0:
                 offs_t = load_list(offs, "offs_t")
         w_raw = []
-        for n, (g, c0, width) in enumerate(W_PIECES):
+        for g in range(PASSES):
             rows = w1[g * K_PASS : (g + 1) * K_PASS, :].rearrange("(p j) c -> p j c", j=PACK)
-            raw = keep.tile([P, PACK, width], F32, name=f"w_raw{n}")
-            nc.sync.dma_start(raw[:], rows[:, :, c0 : c0 + width])
+            raw = keep.tile([P, 2, PACK, W_HALF], F32, name=f"w_raw{g}", tag=f"w_raw{g}", align_bytes=64)
+            for a in range(2):
+                nc.sync.dma_start(raw[:, a], rows[:, :, a * W_HALF : (a + 1) * W_HALF])
             w_raw.append(raw)
         pos_t, gate_t = [], []
         for d, src in enumerate((pos1, pos2)):
@@ -91,7 +92,6 @@ def tile_picked_hop2_relu_e_kernel(
 
         x_words = [keep.tile([P, T], U32, name=f"x_words{g}", align_bytes=64) for g in range(PASSES)]
         halves = S // BANK
-        cols = BANK // STRIPE
         picked0 = keep.tile([P, S], U32, name="picked0", align_bytes=64)
 
         def quantise_chunk(n):
@@ -109,63 +109,94 @@ def tile_picked_hop2_relu_e_kernel(
             x_bf.append(grouped)
             dst = grouped[:].rearrange("p (c i) j -> p c j i", i=4)
             src = raw[:].rearrange("p j (c i) -> p c j i", i=4)
-            nc.scalar.activation(dst[:, : share // 4], src[:, : share // 4], COPY)
-            nc.vector.tensor_copy(dst[:, share // 4 :], src[:, share // 4 :])
+            if share > 0:
+                nc.scalar.activation(dst[:, : share // 4], src[:, : share // 4], COPY)
+            if share < width:
+                nc.vector.tensor_copy(dst[:, share // 4 :], src[:, share // 4 :])
             quantise_chunk(n)
             if n == first_of_pass1:
                 nc.vector.tensor_copy(picked0[:], x_words[0][:].indirect(offs_t[:]))
 
-        w_bf = [keep.tile([P, PACK, P, PACK], BF16, name=f"w_bf{g}", tag=f"w_bf{g}", align_bytes=64) for g in range(PASSES)]
-        w_words = [keep.tile([P, H], U32, name=f"w_words{g}", align_bytes=64) for g in range(PASSES)]
-        w_scales = [keep.tile([P, H], U8, name=f"w_scales{g}", align_bytes=64) for g in range(PASSES)]
+        stationary = {}
+        early = [keep.tile([P, 2, P, PACK], BF16, name=f"w_early{g}", tag=f"w_early{g}", align_bytes=64) for g in range(PASSES)]
+        late = keep.tile([P, PASSES, 2, P, PACK], BF16, name="w_late", align_bytes=64)
 
-        for n, (g, c0, width) in enumerate(W_PIECES):
-            dst = w_bf[g][:, :, c0 // 4 : (c0 + width) // 4, :].rearrange("p t m j -> p m t j")
-            nc.scalar.activation(dst, w_raw[n][:].rearrange("p j (m t) -> p m t j", t=PACK), COPY)
+        def cast_views(g, u, tile):
+            dst = tile.rearrange("p e (a m) j -> p a m j e", a=2)
+            src = w_raw[g][:].rearrange("p a j (m t) -> p a m j t", t=PACK)[:, :, :, :, 2 * u : 2 * u + 2]
+            return dst, src
 
-        picked_scales, picked1 = [], []
+        for g in range(PASSES):
+            dst, src = cast_views(g, 0, early[g][:])
+            for a in range(2):
+                nc.scalar.copy(dst[:, a], src[:, a])
+        dst, src = cast_views(0, 1, late[:, 0])
+        for a in range(2):
+            nc.scalar.copy(dst[:, a], src[:, a])
+        dst, src = cast_views(1, 1, late[:, 1])
+        nc.scalar.copy(dst, src)
 
-        def gather_half(b, tag, word_tag):
-            part = offs_t[:, b * cols : (b + 1) * cols]
-            tile = keep.tile([P, BANK], U8, name=f"picked_scales{b}", tag=tag, align_bytes=64)
-            picked_scales.append(tile)
-            nc.vector.tensor_copy(tile[:], x_scales[:].indirect(part))
-            words = keep.tile([P, BANK], U32, name=f"picked1_{b}", tag=word_tag, align_bytes=64)
+        def quantise_w(name, source, keys):
+            words = keep.tile([P, len(keys) * P], U32, name=f"w_words_{name}", align_bytes=64)
+            scales = keep.tile([P, len(keys) * P], U8, name=f"w_scales_{name}", align_bytes=64)
+            nc.vector.quantize_mx(out=words[:].bitcast(FP8X4), scales=scales[:], in_=source)
+            for n, key in enumerate(keys):
+                stationary[key] = (words[:, n * P : (n + 1) * P], scales[:, n * P : (n + 1) * P])
+
+        picked_scales = keep.tile([P, S], U8, name="picked_scales", align_bytes=64)
+        nc.vector.tensor_copy(picked_scales[:], x_scales[:].indirect(offs_t[:]))
+        picked1 = []
+        cols = BANK // STRIPE
+        for b in range(halves):
+            quantise_w(f"early{b}", early[b][:].rearrange("p e m j -> p (e m j)"), [(b, 0), (b, 1)])
+            words = keep.tile([P, BANK], U32, name=f"picked1_{b}", tag=("w_raw0", "w_early1")[b], align_bytes=64)
+            nc.vector.tensor_copy(words[:], x_words[1][:].indirect(offs_t[:, b * cols : (b + 1) * cols]))
             picked1.append(words)
-            nc.vector.tensor_copy(words[:], x_words[1][:].indirect(part))
-
-        gather_half(0, "picked_scales0", "picked1_0")
-        nc.vector.quantize_mx(
-            out=w_words[0][:].bitcast(FP8X4), scales=w_scales[0][:], in_=w_bf[0][:].rearrange("p t m j -> p (t m j)")
-        )
-        gather_half(1, "w_bf0", "x_scales")
-        for t in range(PACK):
-            nc.vector.quantize_mx(
-                out=w_words[1][:, t * P : (t + 1) * P].bitcast(FP8X4),
-                scales=w_scales[1][:, t * P : (t + 1) * P],
-                in_=w_bf[1][:, t].rearrange("p m j -> p (m j)"),
-            )
+        quantise_w("late", late[:].rearrange("p g e m j -> p (g e m j)"), [(0, 2), (0, 3), (1, 2), (1, 3)])
 
         terms = [keep.tile([P, PACK, V], F32, name=f"terms{d}") for d in range(2)]
-        for t in range(PACK):
+        banks = {}
+
+        def multiply(t, g, b):
+            if g == 0:
+                banks[(t, b)] = psum.tile([P, BANK], F32, name=f"bank{t}_{b}", tag=f"bank{(2 * t + b) % 4}")
+            moving = picked0[:, b * BANK : (b + 1) * BANK] if g == 0 else picked1[b][:]
+            words, scales = stationary[(g, t)]
+            nc.tensor.matmul_mx(
+                out=banks[(t, b)][:],
+                lhsT=words.bitcast(FP8X4),
+                lhsT_scale=scales,
+                rhs=moving.bitcast(FP8X4),
+                rhs_scale=picked_scales[4 * g : P, b * BANK : (b + 1) * BANK],
+                start=(g == 0),
+                stop=(g == PASSES - 1),
+            )
+
+        def first_hop(t):
             h = keep.tile([P, S], F32, name=f"h{t}")
-            banks = [psum.tile([P, BANK], F32, name=f"bank{2 * t + b}", tag=f"bank{(2 * t + b) % 4}") for b in range(halves)]
-            for g in range(PASSES):
-                for b in range(halves):
-                    moving = picked0[:, b * BANK : (b + 1) * BANK] if g == 0 else picked1[b][:]
-                    nc.tensor.matmul_mx(
-                        out=banks[b][:],
-                        lhsT=w_words[g][:, t * P : (t + 1) * P].bitcast(FP8X4),
-                        lhsT_scale=w_scales[g][:, t * P : (t + 1) * P],
-                        rhs=moving.bitcast(FP8X4),
-                        rhs_scale=picked_scales[b][4 * g : P, :],
-                        start=(g == 0),
-                        stop=(g == PASSES - 1),
-                    )
             for b in range(halves):
-                nc.scalar.activation(h[:, b * BANK : (b + 1) * BANK], banks[b][:], RELU)
-            for d in range(2):
-                nc.vector.tensor_tensor(terms[d][:, t, :], h[:].indirect(pos_t[d][:]), gate_t[d][:], MULT)
+                nc.scalar.activation(h[:, b * BANK : (b + 1) * BANK], banks[(t, b)][:], RELU)
+            for v0, width in Z_PIECES if t == PACK - 1 else [(0, V)]:
+                for d in range(2):
+                    part = pos_t[d][:, v0 // STRIPE : (v0 + width) // STRIPE]
+                    nc.vector.tensor_tensor(
+                        terms[d][:, t, v0 : v0 + width], h[:].indirect(part), gate_t[d][:, v0 : v0 + width], MULT
+                    )
+
+        for t in range(2):
+            for b in range(halves):
+                multiply(t, 0, b)
+        for b in range(halves):
+            multiply(0, 1, b)
+        first_hop(0)
+        for b in range(halves):
+            multiply(1, 1, b)
+        first_hop(1)
+        for t in range(2, PACK):
+            for b in range(halves):
+                for g in range(PASSES):
+                    multiply(t, g, b)
+            first_hop(t)
 
         g_rows = [keep.tile([P, V], F32, name=f"g_rows{m}") for m in range(N // P)]
         z_bf = [keep.tile([P, w, PACK], BF16, name=f"z_bf{n}", align_bytes=64) for n, (v0, w) in enumerate(Z_PIECES)]
@@ -191,10 +222,19 @@ def tile_picked_hop2_relu_e_kernel(
                 )
                 nc.scalar.activation(g_rows[m][:, v0 : v0 + width], bank[:, :width], RELU)
 
-        for m in range(N // P):
-            parts = [keep.tile([P, U], F32, name=f"parts{m}_{d}") for d in range(2)]
-            for d in range(2):
-                nc.vector.tensor_tensor(parts[d][:], g_rows[m][:].indirect(nxt_t[d][:]), gate2_t[d][:], MULT)
+        parts = [[keep.tile([P, U], F32, name=f"parts{m}_{d}") for d in range(2)] for m in range(N // P)]
+
+        def fetch(m, d):
+            nc.vector.tensor_tensor(parts[m][d][:], g_rows[m][:].indirect(nxt_t[d][:]), gate2_t[d][:], MULT)
+
+        def finish(m):
             result = keep.tile([P, U], F32, name=f"result{m}")
-            nc.vector.tensor_tensor(result[:], parts[0][:], parts[1][:], ADD)
+            nc.vector.tensor_tensor(result[:], parts[m][0][:], parts[m][1][:], ADD)
             nc.sync.dma_start(out[m * P : (m + 1) * P, :], result[:])
+
+        fetch(0, 0)
+        fetch(0, 1)
+        fetch(1, 0)
+        finish(0)
+        fetch(1, 1)
+        finish(1)

@@ -1,6 +1,7 @@
 from contextlib import ExitStack
 
 import concourse.mybir as mybir
+from concourse.masks import make_identity
 
 K, T, S, V, H, N, U = 1024, 2048, 1024, 512, 512, 256, 256
 FLOPS = 2 * K * H * S + 2 * H * N * V
@@ -24,13 +25,26 @@ K_PASS = P * PACK
 PASSES = K // K_PASS
 BANK = 512
 STRIPE = 16
+HOPS = 2
+ALIGN = 64
 
-X_CHUNKS = [
-    [(512, 256), (512, 256), (512, 256), (512, 160)],
-    [(512, 448), (512, 256), (512, 176), (256, 160), (128, 128), (128, 0)],
+EVEN = 256
+QUICK = 160
+RELIEF = 448
+X_LOADS = [
+    [(512, EVEN), (512, EVEN), (512, EVEN), (512, QUICK)],
+    [(512, RELIEF), (512, EVEN), (512, QUICK), (256, QUICK), (128, 128), (128, 0)],
 ]
 W_HALF = H // 2
-Z_PIECES = [(0, 256), (256, 256)]
+
+TWO_STRETCHES = [(0, BANK), (BANK, BANK)]
+THREE_STRETCHES = [(0, BANK), (BANK, BANK // 2), (BANK + BANK // 2, BANK // 2)]
+STRETCHES = [THREE_STRETCHES, TWO_STRETCHES, TWO_STRETCHES, THREE_STRETCHES]
+EARLY_BANKS = {(0, 0): 0, (0, 1): 1, (0, 2): 2, (1, 0): 3, (1, 1): 4}
+LATE_BANKS = {(2, 0): 0, (3, 0): 1, (3, 1): 3, (2, 1): 4, (3, 2): 0}
+
+Z_HALF = V // 2
+Z_BLOCKS = Z_HALF // P
 
 
 def tile_picked_hop2_relu_e_kernel(
@@ -47,29 +61,34 @@ def tile_picked_hop2_relu_e_kernel(
             nc.sync.dma_start(tile[:], src)
             return tile
 
-        x_scales = keep.tile([P, T], U8, name="x_scales", tag="x_scales", align_bytes=64)
+        def entries(list_tile, first, count):
+            return list_tile[:, first // STRIPE : (first + count) // STRIPE]
+
+        def pass_rows(matrix, g):
+            return matrix[g * K_PASS : (g + 1) * K_PASS, :].rearrange("(p j) c -> p j c", j=PACK)
+
+        x_scales = keep.tile([P, T], U8, name="x_scales", align_bytes=ALIGN)
         nc.gpsimd.memset(x_scales[:], 0)
-        w2_plane = keep.tile([P, N], U8, name="w2_plane", align_bytes=64)
+        w2_plane = keep.tile([P, N], U8, name="w2_plane", align_bytes=ALIGN)
         nc.gpsimd.memset(w2_plane[:], 0)
+        identity = keep.tile([P, P], F32, name="identity")
+        make_identity(nc, identity[:])
 
         x_raw = []
-        offs_t = None
         for g in range(PASSES):
             c0 = 0
-            rows = xT[g * K_PASS : (g + 1) * K_PASS, :].rearrange("(p j) c -> p j c", j=PACK)
-            for n, (width, share) in enumerate(X_CHUNKS[g]):
+            for n, (width, share) in enumerate(X_LOADS[g]):
                 raw = keep.tile([P, PACK, width], F32, name=f"x_raw{g}_{n}")
-                nc.sync.dma_start(raw[:], rows[:, :, c0 : c0 + width])
+                nc.sync.dma_start(raw[:], pass_rows(xT, g)[:, :, c0 : c0 + width])
                 x_raw.append((g, c0, width, share, raw))
                 c0 += width
             if g == 0:
                 offs_t = load_list(offs, "offs_t")
         w_raw = []
         for g in range(PASSES):
-            rows = w1[g * K_PASS : (g + 1) * K_PASS, :].rearrange("(p j) c -> p j c", j=PACK)
-            raw = keep.tile([P, 2, PACK, W_HALF], F32, name=f"w_raw{g}", tag=f"w_raw{g}", align_bytes=64)
+            raw = keep.tile([P, 2, PACK, W_HALF], F32, name=f"w_raw{g}", tag=f"w_raw{g}", align_bytes=ALIGN)
             for a in range(2):
-                nc.sync.dma_start(raw[:, a], rows[:, :, a * W_HALF : (a + 1) * W_HALF])
+                nc.sync.dma_start(raw[:, a], pass_rows(w1, g)[:, :, a * W_HALF : (a + 1) * W_HALF])
             w_raw.append(raw)
         pos_t, gate_t = [], []
         for d, src in enumerate((pos1, pos2)):
@@ -77,7 +96,7 @@ def tile_picked_hop2_relu_e_kernel(
             tile = keep.tile([P, V], F32, name=f"gate_t{d}")
             nc.sync.dma_start(tile[:], gate[d])
             gate_t.append(tile)
-        w2_codes = keep.tile([P, 2 * N], U8, name="w2_codes", align_bytes=64)
+        w2_codes = keep.tile([P, 2 * N], U8, name="w2_codes", align_bytes=ALIGN)
         nc.sync.dma_start(w2_codes[:], w2_words[0])
         for q in range(4):
             nc.sync.dma_start(
@@ -90,129 +109,200 @@ def tile_picked_hop2_relu_e_kernel(
             nc.sync.dma_start(tile[:], gate2[d])
             gate2_t.append(tile)
 
-        x_words = [keep.tile([P, T], U32, name=f"x_words{g}", align_bytes=64) for g in range(PASSES)]
-        halves = S // BANK
-        picked0 = keep.tile([P, S], U32, name="picked0", align_bytes=64)
-
-        def quantise_chunk(n):
-            g, c0, width, share, raw = x_raw[n]
-            nc.vector.quantize_mx(
-                out=x_words[g][:, c0 : c0 + width].bitcast(FP8X4),
-                scales=x_scales[4 * g : P, c0 : c0 + width],
-                in_=x_bf[n][:].rearrange("p c j -> p (c j)"),
-            )
-
-        x_bf = []
-        first_of_pass1 = len(X_CHUNKS[0])
+        x_words = [keep.tile([P, T], U32, name=f"x_words{g}", align_bytes=ALIGN) for g in range(PASSES)]
+        picked0 = keep.tile([P, S], U32, name="picked0", align_bytes=ALIGN)
         for n, (g, c0, width, share, raw) in enumerate(x_raw):
-            grouped = keep.tile([P, width, PACK], BF16, name=f"x_bf{n}", align_bytes=64)
-            x_bf.append(grouped)
+            grouped = keep.tile([P, width, PACK], BF16, name=f"x_bf{n}", align_bytes=ALIGN)
             dst = grouped[:].rearrange("p (c i) j -> p c j i", i=4)
             src = raw[:].rearrange("p j (c i) -> p c j i", i=4)
             if share > 0:
                 nc.scalar.activation(dst[:, : share // 4], src[:, : share // 4], COPY)
             if share < width:
                 nc.vector.tensor_copy(dst[:, share // 4 :], src[:, share // 4 :])
-            quantise_chunk(n)
-            if n == first_of_pass1:
+            nc.vector.quantize_mx(
+                out=x_words[g][:, c0 : c0 + width].bitcast(FP8X4),
+                scales=x_scales[4 * g : P, c0 : c0 + width],
+                in_=grouped[:].rearrange("p c j -> p (c j)"),
+            )
+            if (g, c0) == (1, 0):
                 nc.vector.tensor_copy(picked0[:], x_words[0][:].indirect(offs_t[:]))
 
-        stationary = {}
-        early = [keep.tile([P, 2, P, PACK], BF16, name=f"w_early{g}", tag=f"w_early{g}", align_bytes=64) for g in range(PASSES)]
-        late = keep.tile([P, PASSES, 2, P, PACK], BF16, name="w_late", align_bytes=64)
+        early = [
+            keep.tile([P, 2, P, PACK], BF16, name=f"w_early{g}", tag=f"w_early{g}", align_bytes=ALIGN)
+            for g in range(PASSES)
+        ]
+        late = keep.tile([P, PASSES, 2, P, PACK], BF16, name="w_late", align_bytes=ALIGN)
 
-        def cast_views(g, u, tile):
+        def deal_views(g, u, tile):
             dst = tile.rearrange("p e (a m) j -> p a m j e", a=2)
             src = w_raw[g][:].rearrange("p a j (m t) -> p a m j t", t=PACK)[:, :, :, :, 2 * u : 2 * u + 2]
             return dst, src
 
         for g in range(PASSES):
-            dst, src = cast_views(g, 0, early[g][:])
+            dst, src = deal_views(g, 0, early[g][:])
             for a in range(2):
                 nc.scalar.copy(dst[:, a], src[:, a])
-        dst, src = cast_views(0, 1, late[:, 0])
+        dst, src = deal_views(0, 1, late[:, 0])
         for a in range(2):
             nc.scalar.copy(dst[:, a], src[:, a])
-        dst, src = cast_views(1, 1, late[:, 1])
+        dst, src = deal_views(1, 1, late[:, 1])
         nc.scalar.copy(dst, src)
 
+        stationary = {}
+
         def quantise_w(name, source, keys):
-            words = keep.tile([P, len(keys) * P], U32, name=f"w_words_{name}", align_bytes=64)
-            scales = keep.tile([P, len(keys) * P], U8, name=f"w_scales_{name}", align_bytes=64)
+            words = keep.tile([P, len(keys) * P], U32, name=f"w_words_{name}", align_bytes=ALIGN)
+            scales = keep.tile([P, len(keys) * P], U8, name=f"w_scales_{name}", align_bytes=ALIGN)
             nc.vector.quantize_mx(out=words[:].bitcast(FP8X4), scales=scales[:], in_=source)
             for n, key in enumerate(keys):
                 stationary[key] = (words[:, n * P : (n + 1) * P], scales[:, n * P : (n + 1) * P])
 
-        picked_scales = keep.tile([P, S], U8, name="picked_scales", align_bytes=64)
+        def quantise_early(g):
+            quantise_w(f"early{g}", early[g][:].rearrange("p e m j -> p (e m j)"), [(g, 0), (g, 1)])
+
+        def gather_pass1(name, tag, stretches):
+            words = keep.tile([P, BANK], U32, name=name, tag=tag, align_bytes=ALIGN)
+            for first, count in stretches:
+                nc.vector.tensor_copy(
+                    words[:, first % BANK : first % BANK + count],
+                    x_words[1][:].indirect(entries(offs_t, first, count)),
+                )
+            return words
+
+        picked_scales = keep.tile([P, S], U8, name="picked_scales", align_bytes=ALIGN)
         nc.vector.tensor_copy(picked_scales[:], x_scales[:].indirect(offs_t[:]))
-        picked1 = []
-        cols = BANK // STRIPE
-        for b in range(halves):
-            quantise_w(f"early{b}", early[b][:].rearrange("p e m j -> p (e m j)"), [(b, 0), (b, 1)])
-            words = keep.tile([P, BANK], U32, name=f"picked1_{b}", tag=("w_raw0", "w_early1")[b], align_bytes=64)
-            nc.vector.tensor_copy(words[:], x_words[1][:].indirect(offs_t[:, b * cols : (b + 1) * cols]))
-            picked1.append(words)
-        quantise_w("late", late[:].rearrange("p g e m j -> p (g e m j)"), [(0, 2), (0, 3), (1, 2), (1, 3)])
+        quantise_early(0)
+        picked1 = [gather_pass1("picked1_0", "w_raw0", THREE_STRETCHES[:1])]
+        quantise_early(1)
+        picked1.append(gather_pass1("picked1_1", "w_early1", THREE_STRETCHES[1:]))
+        late_keys = [(g, t) for g in range(PASSES) for t in (2, 3)]
+        quantise_w("late", late[:].rearrange("p g e m j -> p (g e m j)"), late_keys)
 
-        terms = [keep.tile([P, PACK, V], F32, name=f"terms{d}") for d in range(2)]
-        banks = {}
+        terms = [keep.tile([P, PACK, V], F32, name=f"terms{d}") for d in range(HOPS)]
+        h_rows = [keep.tile([P, S], F32, name=f"h{t}") for t in range(PACK)]
+        bank_of = EARLY_BANKS | LATE_BANKS
+        groups = {}
 
-        def multiply(t, g, b):
+        def multiply(t, g, n):
+            first, count = STRETCHES[t][n]
             if g == 0:
-                banks[(t, b)] = psum.tile([P, BANK], F32, name=f"bank{t}_{b}", tag=f"bank{(2 * t + b) % 4}")
-            moving = picked0[:, b * BANK : (b + 1) * BANK] if g == 0 else picked1[b][:]
+                groups[(t, n)] = psum.tile([P, BANK], F32, name=f"h_bank{t}_{n}", tag=f"bank{bank_of[(t, n)]}")
+                moving = picked0[:, first : first + count]
+            else:
+                moving = picked1[first // BANK][:, first % BANK : first % BANK + count]
             words, scales = stationary[(g, t)]
             nc.tensor.matmul_mx(
-                out=banks[(t, b)][:],
+                out=groups[(t, n)][:, :count],
                 lhsT=words.bitcast(FP8X4),
                 lhsT_scale=scales,
                 rhs=moving.bitcast(FP8X4),
-                rhs_scale=picked_scales[4 * g : P, b * BANK : (b + 1) * BANK],
+                rhs_scale=picked_scales[4 * g : P, first : first + count],
                 start=(g == 0),
                 stop=(g == PASSES - 1),
             )
 
-        def first_hop(t):
-            h = keep.tile([P, S], F32, name=f"h{t}")
-            for b in range(halves):
-                nc.scalar.activation(h[:, b * BANK : (b + 1) * BANK], banks[(t, b)][:], RELU)
-            for v0, width in Z_PIECES if t == PACK - 1 else [(0, V)]:
-                for d in range(2):
-                    part = pos_t[d][:, v0 // STRIPE : (v0 + width) // STRIPE]
-                    nc.vector.tensor_tensor(
-                        terms[d][:, t, v0 : v0 + width], h[:].indirect(part), gate_t[d][:, v0 : v0 + width], MULT
-                    )
+        def leave_bank(t, n):
+            first, count = STRETCHES[t][n]
+            nc.scalar.activation(h_rows[t][:, first : first + count], groups[(t, n)][:, :count], RELU)
 
-        for t in range(2):
-            for b in range(halves):
-                multiply(t, 0, b)
-        for b in range(halves):
-            multiply(0, 1, b)
-        first_hop(0)
-        for b in range(halves):
-            multiply(1, 1, b)
-        first_hop(1)
-        for t in range(2, PACK):
-            for b in range(halves):
-                for g in range(PASSES):
-                    multiply(t, g, b)
-            first_hop(t)
+        def weigh(t, d, v0, width):
+            nc.vector.tensor_tensor(
+                terms[d][:, t, v0 : v0 + width],
+                h_rows[t][:].indirect(entries(pos_t[d], v0, width)),
+                gate_t[d][:, v0 : v0 + width],
+                MULT,
+            )
+
+        for t, n in EARLY_BANKS:
+            multiply(t, 0, n)
+        for t in (0, 1):
+            for n in range(len(STRETCHES[t])):
+                multiply(t, 1, n)
+            for n in range(len(STRETCHES[t])):
+                leave_bank(t, n)
+            for d in range(HOPS):
+                weigh(t, d, 0, V)
+        for t, n in LATE_BANKS:
+            for g in range(PASSES):
+                multiply(t, g, n)
+            leave_bank(t, n)
+        for t in (2, 3):
+            for d in range(HOPS):
+                weigh(t, d, 0, Z_HALF)
+
+        first_sums = psum.tile([P, Z_BLOCKS, 2, P], F32, name="first_sums", tag="bank4")
+        sums = {(0, b): first_sums[:, b] for b in range(Z_BLOCKS)}
+        for b, bank in enumerate((0, 7)):
+            sums[(1, b)] = psum.tile([P, 2, P], F32, name=f"last_sums{b}", tag=f"bank{bank}")[:]
+        back = [psum.tile([P, 2, P], F32, name=f"back{b}", tag=f"bank{5 + b}") for b in range(Z_BLOCKS)]
+        turned = {}
+
+        def turn(t, b, d):
+            nc.tensor.matmul(
+                sums[(t // 2, b)][:, t % 2, :],
+                lhsT=terms[d][:, t, b * P : (b + 1) * P],
+                rhs=identity[:],
+                start=(d == 0),
+                stop=(d == HOPS - 1),
+                is_transpose=True,
+            )
+
+        def round_sums(u, b):
+            tile = keep.tile([P, P, 2], BF16, name=f"turned{u}_{b}", tag=f"turned{u}_{b}", align_bytes=ALIGN)
+            nc.scalar.copy(tile[:], sums[(u, b)].rearrange("v e m -> v m e"))
+            turned[(u, b)] = tile
+
+        for t in (0, 1):
+            for b in range(Z_BLOCKS):
+                for d in range(HOPS):
+                    turn(t, b, d)
+        for b in range(Z_BLOCKS):
+            round_sums(0, b)
+        for t in (2, 3):
+            for d in range(HOPS):
+                for b in range(Z_BLOCKS):
+                    turn(t, b, d)
+        for b in range(Z_BLOCKS):
+            round_sums(1, b)
+        for u in range(2):
+            for b in range(Z_BLOCKS):
+                words = turned[(u, b)][:].rearrange("v m e -> v (m e)").bitcast(F32)
+                nc.tensor.transpose(back[b][:, u, :], words, identity[:])
 
         g_rows = [keep.tile([P, V], F32, name=f"g_rows{m}") for m in range(N // P)]
-        z_bf = [keep.tile([P, w, PACK], BF16, name=f"z_bf{n}", align_bytes=64) for n, (v0, w) in enumerate(Z_PIECES)]
-        for n, (v0, width) in enumerate(Z_PIECES):
-            views = [terms[d][:, :, v0 : v0 + width].rearrange("p t (c i) -> p c t i", i=4) for d in range(2)]
-            nc.vector.tensor_tensor(z_bf[n][:].rearrange("p (c i) t -> p c t i", i=4), views[0], views[1], ADD)
-        for n, (v0, width) in enumerate(Z_PIECES):
-            z_words = keep.tile([P, width], U32, name=f"z_words{n}", align_bytes=64)
-            z_scales = keep.tile([P, width], U8, name=f"z_scales{n}", align_bytes=64)
+        z_bf = [
+            keep.tile([P, Z_HALF, PACK], BF16, name=f"z_bf{n}", tag=tag, align_bytes=ALIGN)
+            for n, tag in enumerate(("z_bf0", "turned1_0"))
+        ]
+        pairs = z_bf[0][:].rearrange("p v t -> p (v t)").bitcast(F32)
+        pairs = pairs.rearrange("p (b v u) -> p b v u", b=Z_BLOCKS, u=2)
+        for b in range(Z_BLOCKS):
+            nc.scalar.copy(pairs[:, b], back[b][:].rearrange("p u v -> p v u"))
+
+        for d in range(HOPS):
+            weigh(2, d, Z_HALF, Z_HALF)
+        weigh(3, 0, Z_HALF, Z_HALF)
+        for v0 in range(Z_HALF, V, P):
+            weigh(3, 1, v0, P)
+        for v0 in range(Z_HALF, V, P):
+            views = [terms[d][:, :, v0 : v0 + P].rearrange("p t (c i) -> p c t i", i=2) for d in range(HOPS)]
+            dst = z_bf[1][:, v0 - Z_HALF : v0 - Z_HALF + P, :].rearrange("p (c i) t -> p c t i", i=2)
+            nc.vector.tensor_tensor(dst, views[0], views[1], ADD)
+
+        z_codes = []
+        for n in range(2):
+            z_words = keep.tile([P, Z_HALF], U32, name=f"z_words{n}", align_bytes=ALIGN)
+            z_scales = keep.tile([P, Z_HALF], U8, name=f"z_scales{n}", align_bytes=ALIGN)
             nc.vector.quantize_mx(
                 out=z_words[:].bitcast(FP8X4), scales=z_scales[:], in_=z_bf[n][:].rearrange("p v t -> p (v t)")
             )
-            for m in range(N // P):
-                bank = psum.tile([P, BANK], F32, name=f"g_bank{2 * n + m}", tag=f"bank{4 + 2 * n + m}")
+            z_codes.append((z_words, z_scales))
+        for m in range(N // P):
+            for n in range(2):
+                bank = psum.tile([P, BANK], F32, name=f"g_bank{n}_{m}", tag=f"bank{1 if n == 0 else 2 + m}")
+                z_words, z_scales = z_codes[n]
                 nc.tensor.matmul_mx(
-                    out=bank[:, :width],
+                    out=bank[:, :Z_HALF],
                     lhsT=w2_codes[:, 2 * P * m : 2 * P * (m + 1)].bitcast(FP4X4),
                     lhsT_scale=w2_plane[:, P * m : P * (m + 1)],
                     rhs=z_words[:].bitcast(FP8X4),
@@ -220,21 +310,17 @@ def tile_picked_hop2_relu_e_kernel(
                     start=True,
                     stop=True,
                 )
-                nc.scalar.activation(g_rows[m][:, v0 : v0 + width], bank[:, :width], RELU)
+                dst = g_rows[m][:, n * Z_HALF : (n + 1) * Z_HALF]
+                if (n, m) == (1, 0):
+                    nc.vector.tensor_scalar_max(dst, bank[:, :Z_HALF], 0.0)
+                else:
+                    nc.scalar.activation(dst, bank[:, :Z_HALF], RELU)
 
-        parts = [[keep.tile([P, U], F32, name=f"parts{m}_{d}") for d in range(2)] for m in range(N // P)]
-
-        def fetch(m, d):
-            nc.vector.tensor_tensor(parts[m][d][:], g_rows[m][:].indirect(nxt_t[d][:]), gate2_t[d][:], MULT)
-
-        def finish(m):
+        parts = [[keep.tile([P, U], F32, name=f"parts{m}_{d}") for d in range(HOPS)] for m in range(N // P)]
+        for m in range(N // P):
+            for d in range(HOPS):
+                nc.vector.tensor_tensor(parts[m][d][:], g_rows[m][:].indirect(nxt_t[d][:]), gate2_t[d][:], MULT)
+        for m in range(N // P):
             result = keep.tile([P, U], F32, name=f"result{m}")
             nc.vector.tensor_tensor(result[:], parts[m][0][:], parts[m][1][:], ADD)
             nc.sync.dma_start(out[m * P : (m + 1) * P, :], result[:])
-
-        fetch(0, 0)
-        fetch(0, 1)
-        fetch(1, 0)
-        finish(0)
-        fetch(1, 1)
-        finish(1)

@@ -33,18 +33,20 @@ QUICK = 160
 RELIEF = 448
 X_LOADS = [
     [(512, EVEN), (512, EVEN), (512, EVEN), (512, QUICK)],
-    [(512, RELIEF), (512, EVEN), (512, QUICK), (256, QUICK), (128, 128), (128, 0)],
+    [(512, RELIEF), (512, 320), (256, 128), (256, 128), (256, 128), (128, 96), (128, 32)],
 ]
 W_HALF = H // 2
 
 TWO_STRETCHES = [(0, BANK), (BANK, BANK)]
 THREE_STRETCHES = [(0, BANK), (BANK, BANK // 2), (BANK + BANK // 2, BANK // 2)]
+HEAD = 3 * BANK // 2
 STRETCHES = [THREE_STRETCHES, TWO_STRETCHES, TWO_STRETCHES, THREE_STRETCHES]
 EARLY_BANKS = {(0, 0): 0, (0, 1): 1, (0, 2): 2, (1, 0): 3, (1, 1): 4}
 LATE_BANKS = {(2, 0): 0, (3, 0): 1, (3, 1): 3, (2, 1): 4, (3, 2): 0}
 
-Z_HALF = V // 2
-Z_BLOCKS = Z_HALF // P
+Z_GROUPS = [(0, 2 * P), (2 * P, P), (3 * P, P)]
+TURNED_BLOCKS = 3
+G_BANKS = [(3, 4), (0, 7), (2, 1)]
 
 
 def tile_picked_hop2_relu_e_kernel(
@@ -160,21 +162,16 @@ def tile_picked_hop2_relu_e_kernel(
         def quantise_early(g):
             quantise_w(f"early{g}", early[g][:].rearrange("p e m j -> p (e m j)"), [(g, 0), (g, 1)])
 
-        def gather_pass1(name, tag, stretches):
-            words = keep.tile([P, BANK], U32, name=name, tag=tag, align_bytes=ALIGN)
-            for first, count in stretches:
-                nc.vector.tensor_copy(
-                    words[:, first % BANK : first % BANK + count],
-                    x_words[1][:].indirect(entries(offs_t, first, count)),
-                )
-            return words
-
         picked_scales = keep.tile([P, S], U8, name="picked_scales", align_bytes=ALIGN)
         nc.vector.tensor_copy(picked_scales[:], x_scales[:].indirect(offs_t[:]))
         quantise_early(0)
-        picked1 = [gather_pass1("picked1_0", "w_raw0", THREE_STRETCHES[:1])]
+        head = keep.tile([P, HEAD], U32, name="picked1_head", tag="w_raw0", align_bytes=ALIGN)
+        for first, count in THREE_STRETCHES[:2]:
+            nc.vector.tensor_copy(head[:, first : first + count], x_words[1][:].indirect(entries(offs_t, first, count)))
         quantise_early(1)
-        picked1.append(gather_pass1("picked1_1", "w_early1", THREE_STRETCHES[1:]))
+        first, count = THREE_STRETCHES[2]
+        tail = keep.tile([P, count], U32, name="picked1_tail", tag="w_early1", align_bytes=ALIGN)
+        nc.vector.tensor_copy(tail[:], x_words[1][:].indirect(entries(offs_t, first, count)))
         late_keys = [(g, t) for g in range(PASSES) for t in (2, 3)]
         quantise_w("late", late[:].rearrange("p g e m j -> p (g e m j)"), late_keys)
 
@@ -187,23 +184,32 @@ def tile_picked_hop2_relu_e_kernel(
             first, count = STRETCHES[t][n]
             if g == 0:
                 groups[(t, n)] = psum.tile([P, BANK], F32, name=f"h_bank{t}_{n}", tag=f"bank{bank_of[(t, n)]}")
-                moving = picked0[:, first : first + count]
+                pieces = [(first, count, picked0[:, first : first + count])]
             else:
-                moving = picked1[first // BANK][:, first % BANK : first % BANK + count]
+                pieces = [
+                    (f, c, head[:, f : f + c] if f + c <= HEAD else tail[:])
+                    for f, c in THREE_STRETCHES
+                    if first <= f < first + count
+                ]
             words, scales = stationary[(g, t)]
-            nc.tensor.matmul_mx(
-                out=groups[(t, n)][:, :count],
-                lhsT=words.bitcast(FP8X4),
-                lhsT_scale=scales,
-                rhs=moving.bitcast(FP8X4),
-                rhs_scale=picked_scales[4 * g : P, first : first + count],
-                start=(g == 0),
-                stop=(g == PASSES - 1),
-            )
+            for f, c, moving in pieces:
+                nc.tensor.matmul_mx(
+                    out=groups[(t, n)][:, f - first : f - first + c],
+                    lhsT=words.bitcast(FP8X4),
+                    lhsT_scale=scales,
+                    rhs=moving.bitcast(FP8X4),
+                    rhs_scale=picked_scales[4 * g : P, f : f + c],
+                    start=(g == 0),
+                    stop=(g == PASSES - 1 and f + c == first + count),
+                )
 
         def leave_bank(t, n):
             first, count = STRETCHES[t][n]
-            nc.scalar.activation(h_rows[t][:, first : first + count], groups[(t, n)][:, :count], RELU)
+            dst = h_rows[t][:, first : first + count]
+            if (t, n) == (0, 1):
+                nc.vector.tensor_scalar_max(dst, groups[(t, n)][:, :count], 0.0)
+            else:
+                nc.scalar.activation(dst, groups[(t, n)][:, :count], RELU)
 
         def weigh(t, d, v0, width):
             nc.vector.tensor_tensor(
@@ -226,16 +232,18 @@ def tile_picked_hop2_relu_e_kernel(
             for g in range(PASSES):
                 multiply(t, g, n)
             leave_bank(t, n)
-        for t in (2, 3):
-            for d in range(HOPS):
-                weigh(t, d, 0, Z_HALF)
+        for v0, width in Z_GROUPS:
+            for t in (2, 3):
+                for d in range(HOPS):
+                    weigh(t, d, v0, width)
 
-        first_sums = psum.tile([P, Z_BLOCKS, 2, P], F32, name="first_sums", tag="bank4")
-        sums = {(0, b): first_sums[:, b] for b in range(Z_BLOCKS)}
-        for b, bank in enumerate((0, 7)):
-            sums[(1, b)] = psum.tile([P, 2, P], F32, name=f"last_sums{b}", tag=f"bank{bank}")[:]
-        back = [psum.tile([P, 2, P], F32, name=f"back{b}", tag=f"bank{5 + b}") for b in range(Z_BLOCKS)]
-        turned = {}
+        first_sums = psum.tile([P, 2, 2, P], F32, name="first_sums", tag="bank4")
+        sums = {(0, b): first_sums[:, b] for b in range(2)}
+        for (u, b), bank in {(0, 2): 0, (1, 0): 7, (1, 1): 2, (1, 2): 1}.items():
+            sums[(u, b)] = psum.tile([P, 2, P], F32, name=f"sums{u}_{b}", tag=f"bank{bank}")[:]
+        back01 = psum.tile([P, 2, 2, P], F32, name="back01", tag="bank5")
+        back2 = psum.tile([P, 2, P], F32, name="back2", tag="bank6")
+        back = [back01[:, 0], back01[:, 1], back2[:]]
 
         def turn(t, b, d):
             nc.tensor.matmul(
@@ -247,62 +255,61 @@ def tile_picked_hop2_relu_e_kernel(
                 is_transpose=True,
             )
 
-        def round_sums(u, b):
-            tile = keep.tile([P, P, 2], BF16, name=f"turned{u}_{b}", tag=f"turned{u}_{b}", align_bytes=ALIGN)
+        def round_and_turn_back(u, b):
+            tile = keep.tile([P, P, 2], BF16, name=f"turned{u}_{b}", align_bytes=ALIGN)
             nc.scalar.copy(tile[:], sums[(u, b)].rearrange("v e m -> v m e"))
-            turned[(u, b)] = tile
+            words = tile[:].rearrange("v m e -> v (m e)").bitcast(F32)
+            nc.tensor.transpose(back[b][:, u, :], words, identity[:])
 
         for t in (0, 1):
-            for b in range(Z_BLOCKS):
+            for b in range(TURNED_BLOCKS):
                 for d in range(HOPS):
                     turn(t, b, d)
-        for b in range(Z_BLOCKS):
-            round_sums(0, b)
-        for t in (2, 3):
-            for d in range(HOPS):
-                for b in range(Z_BLOCKS):
-                    turn(t, b, d)
-        for b in range(Z_BLOCKS):
-            round_sums(1, b)
-        for u in range(2):
-            for b in range(Z_BLOCKS):
-                words = turned[(u, b)][:].rearrange("v m e -> v (m e)").bitcast(F32)
-                nc.tensor.transpose(back[b][:, u, :], words, identity[:])
+        for b in range(TURNED_BLOCKS):
+            round_and_turn_back(0, b)
+        for blocks in ((0, 1), (2,)):
+            for t in (2, 3):
+                for d in range(HOPS):
+                    for b in blocks:
+                        turn(t, b, d)
+            for b in blocks:
+                round_and_turn_back(1, b)
 
-        g_rows = [keep.tile([P, V], F32, name=f"g_rows{m}") for m in range(N // P)]
-        z_bf = [
-            keep.tile([P, Z_HALF, PACK], BF16, name=f"z_bf{n}", tag=tag, align_bytes=ALIGN)
-            for n, tag in enumerate(("z_bf0", "turned1_0"))
-        ]
-        pairs = z_bf[0][:].rearrange("p v t -> p (v t)").bitcast(F32)
-        pairs = pairs.rearrange("p (b v u) -> p b v u", b=Z_BLOCKS, u=2)
-        for b in range(Z_BLOCKS):
-            nc.scalar.copy(pairs[:, b], back[b][:].rearrange("p u v -> p v u"))
-
-        for d in range(HOPS):
-            weigh(2, d, Z_HALF, Z_HALF)
-        weigh(3, 0, Z_HALF, Z_HALF)
-        for v0 in range(Z_HALF, V, P):
-            weigh(3, 1, v0, P)
-        for v0 in range(Z_HALF, V, P):
-            views = [terms[d][:, :, v0 : v0 + P].rearrange("p t (c i) -> p c t i", i=2) for d in range(HOPS)]
-            dst = z_bf[1][:, v0 - Z_HALF : v0 - Z_HALF + P, :].rearrange("p (c i) t -> p c t i", i=2)
-            nc.vector.tensor_tensor(dst, views[0], views[1], ADD)
+        z01 = keep.tile([P, 2 * P, PACK], BF16, name="z01", align_bytes=ALIGN)
+        z2 = keep.tile([P, P, PACK], BF16, name="z2", align_bytes=ALIGN)
+        pairs = z01[:].rearrange("p v t -> p (v t)").bitcast(F32).rearrange("p (b v u) -> p b v u", b=2, u=2)
+        nc.scalar.copy(pairs, back01[:].rearrange("p b u v -> p b v u"))
+        pairs = z2[:].rearrange("p v t -> p (v t)").bitcast(F32).rearrange("p (v u) -> p v u", u=2)
+        nc.scalar.copy(pairs, back2[:].rearrange("p u v -> p v u"))
 
         z_codes = []
-        for n in range(2):
-            z_words = keep.tile([P, Z_HALF], U32, name=f"z_words{n}", align_bytes=ALIGN)
-            z_scales = keep.tile([P, Z_HALF], U8, name=f"z_scales{n}", align_bytes=ALIGN)
-            nc.vector.quantize_mx(
-                out=z_words[:].bitcast(FP8X4), scales=z_scales[:], in_=z_bf[n][:].rearrange("p v t -> p (v t)")
-            )
+        for n, (v0, width) in enumerate(Z_GROUPS):
+            z_words = keep.tile([P, width], U32, name=f"z_words{n}", align_bytes=ALIGN)
+            z_scales = keep.tile([P, width], U8, name=f"z_scales{n}", align_bytes=ALIGN)
             z_codes.append((z_words, z_scales))
-        for m in range(N // P):
-            for n in range(2):
-                bank = psum.tile([P, BANK], F32, name=f"g_bank{n}_{m}", tag=f"bank{1 if n == 0 else 2 + m}")
+
+        def quantise_z(n, c0, source):
+            z_words, z_scales = z_codes[n]
+            nc.vector.quantize_mx(
+                out=z_words[:, c0 : c0 + P].bitcast(FP8X4),
+                scales=z_scales[:, c0 : c0 + P],
+                in_=source.rearrange("p v t -> p (v t)"),
+            )
+
+        quantise_z(0, 0, z01[:, :P])
+        quantise_z(0, P, z01[:, P:])
+        views = [terms[d][:, :, 3 * P :].rearrange("p t (c i) -> p c t i", i=2) for d in range(HOPS)]
+        nc.vector.tensor_tensor(z01[:, :P].rearrange("p (c i) t -> p c t i", i=2), views[0], views[1], ADD)
+        quantise_z(1, 0, z2[:])
+        quantise_z(2, 0, z01[:, :P])
+
+        g_rows = [keep.tile([P, V], F32, name=f"g_rows{m}") for m in range(N // P)]
+        for n, (v0, width) in enumerate(Z_GROUPS):
+            for m in range(N // P):
+                bank = psum.tile([P, BANK], F32, name=f"g_bank{n}_{m}", tag=f"bank{G_BANKS[n][m]}")
                 z_words, z_scales = z_codes[n]
                 nc.tensor.matmul_mx(
-                    out=bank[:, :Z_HALF],
+                    out=bank[:, :width],
                     lhsT=w2_codes[:, 2 * P * m : 2 * P * (m + 1)].bitcast(FP4X4),
                     lhsT_scale=w2_plane[:, P * m : P * (m + 1)],
                     rhs=z_words[:].bitcast(FP8X4),
@@ -310,11 +317,8 @@ def tile_picked_hop2_relu_e_kernel(
                     start=True,
                     stop=True,
                 )
-                dst = g_rows[m][:, n * Z_HALF : (n + 1) * Z_HALF]
-                if (n, m) == (1, 0):
-                    nc.vector.tensor_scalar_max(dst, bank[:, :Z_HALF], 0.0)
-                else:
-                    nc.scalar.activation(dst, bank[:, :Z_HALF], RELU)
+                dst = g_rows[m][:, v0 : v0 + width]
+                nc.scalar.activation(dst, bank[:, :width], RELU)
 
         parts = [[keep.tile([P, U], F32, name=f"parts{m}_{d}") for d in range(HOPS)] for m in range(N // P)]
         for m in range(N // P):

@@ -1,3 +1,4 @@
+import math
 from contextlib import ExitStack
 
 import concourse.mybir as mybir
@@ -32,10 +33,10 @@ EVEN = 256
 QUICK = 160
 RELIEF = 448
 X_LOADS = [
-    [(512, EVEN), (512, EVEN), (512, EVEN), (512, QUICK)],
+    [(1024, 448), (512, EVEN), (512, QUICK)],
     [(512, RELIEF), (512, 320), (256, 128), (256, 128), (256, 128), (128, 96), (128, 32)],
 ]
-W_HALF = H // 2
+W_LOADS = [(0, 0, 256, "w_first"), (0, 256, 256, "w_raw0"), (1, 0, 384, "w_third"), (1, 384, 128, "w_last")]
 
 TWO_STRETCHES = [(0, BANK), (BANK, BANK)]
 THREE_STRETCHES = [(0, BANK), (BANK, BANK // 2), (BANK + BANK // 2, BANK // 2)]
@@ -46,7 +47,7 @@ LATE_BANKS = {(2, 0): 0, (3, 0): 1, (3, 1): 3, (2, 1): 4, (3, 2): 0}
 
 Z_GROUPS = [(0, 2 * P), (2 * P, P), (3 * P, P)]
 TURNED_BLOCKS = 3
-G_BANKS = [(3, 4), (0, 7), (2, 1)]
+G_BANKS = [(4, 0), (7, 2), (5, 1)]
 
 
 def tile_picked_hop2_relu_e_kernel(
@@ -87,11 +88,10 @@ def tile_picked_hop2_relu_e_kernel(
             if g == 0:
                 offs_t = load_list(offs, "offs_t")
         w_raw = []
-        for g in range(PASSES):
-            raw = keep.tile([P, 2, PACK, W_HALF], F32, name=f"w_raw{g}", tag=f"w_raw{g}", align_bytes=ALIGN)
-            for a in range(2):
-                nc.sync.dma_start(raw[:, a], pass_rows(w1, g)[:, :, a * W_HALF : (a + 1) * W_HALF])
-            w_raw.append(raw)
+        for g, c0, width, tag in W_LOADS:
+            raw = keep.tile([P, PACK, width], F32, name=f"w_raw{g}_{c0}", tag=tag, align_bytes=ALIGN)
+            nc.sync.dma_start(raw[:], pass_rows(w1, g)[:, :, c0 : c0 + width])
+            w_raw.append((g, c0, width, raw))
         pos_t, gate_t = [], []
         for d, src in enumerate((pos1, pos2)):
             pos_t.append(load_list(src, f"pos_t{d}"))
@@ -121,11 +121,15 @@ def tile_picked_hop2_relu_e_kernel(
                 nc.scalar.activation(dst[:, : share // 4], src[:, : share // 4], COPY)
             if share < width:
                 nc.vector.tensor_copy(dst[:, share // 4 :], src[:, share // 4 :])
-            nc.vector.quantize_mx(
-                out=x_words[g][:, c0 : c0 + width].bitcast(FP8X4),
-                scales=x_scales[4 * g : P, c0 : c0 + width],
-                in_=grouped[:].rearrange("p c j -> p (c j)"),
-            )
+            q0 = 0
+            while q0 < width:
+                count = min(BANK, 2 ** int(math.log2(width - q0)))
+                nc.vector.quantize_mx(
+                    out=x_words[g][:, c0 + q0 : c0 + q0 + count].bitcast(FP8X4),
+                    scales=x_scales[4 - 4 * g : P, c0 + q0 : c0 + q0 + count],
+                    in_=grouped[:, q0 : q0 + count].rearrange("p c j -> p (c j)"),
+                )
+                q0 += count
             if (g, c0) == (1, 0):
                 nc.vector.tensor_copy(picked0[:], x_words[0][:].indirect(offs_t[:]))
 
@@ -135,20 +139,17 @@ def tile_picked_hop2_relu_e_kernel(
         ]
         late = keep.tile([P, PASSES, 2, P, PACK], BF16, name="w_late", align_bytes=ALIGN)
 
-        def deal_views(g, u, tile):
-            dst = tile.rearrange("p e (a m) j -> p a m j e", a=2)
-            src = w_raw[g][:].rearrange("p a j (m t) -> p a m j t", t=PACK)[:, :, :, :, 2 * u : 2 * u + 2]
-            return dst, src
+        def deal(load, u):
+            g, c0, width, raw = w_raw[load]
+            tile = early[g][:] if u == 0 else late[:, g]
+            dst = tile.rearrange("p e m j -> p m j e")[:, c0 // PACK : (c0 + width) // PACK]
+            src = raw[:].rearrange("p j (m t) -> p m j t", t=PACK)[:, :, :, 2 * u : 2 * u + 2]
+            nc.scalar.copy(dst, src)
 
-        for g in range(PASSES):
-            dst, src = deal_views(g, 0, early[g][:])
-            for a in range(2):
-                nc.scalar.copy(dst[:, a], src[:, a])
-        dst, src = deal_views(0, 1, late[:, 0])
-        for a in range(2):
-            nc.scalar.copy(dst[:, a], src[:, a])
-        dst, src = deal_views(1, 1, late[:, 1])
-        nc.scalar.copy(dst, src)
+        for load in range(len(W_LOADS)):
+            deal(load, 0)
+        for load in (0, 1, 3, 2):
+            deal(load, 1)
 
         stationary = {}
 
@@ -170,7 +171,7 @@ def tile_picked_hop2_relu_e_kernel(
             nc.vector.tensor_copy(head[:, first : first + count], x_words[1][:].indirect(entries(offs_t, first, count)))
         quantise_early(1)
         first, count = THREE_STRETCHES[2]
-        tail = keep.tile([P, count], U32, name="picked1_tail", tag="w_early1", align_bytes=ALIGN)
+        tail = keep.tile([P, count], U32, name="picked1_tail", tag="w_last", align_bytes=ALIGN)
         nc.vector.tensor_copy(tail[:], x_words[1][:].indirect(entries(offs_t, first, count)))
         late_keys = [(g, t) for g in range(PASSES) for t in (2, 3)]
         quantise_w("late", late[:].rearrange("p g e m j -> p (g e m j)"), late_keys)
@@ -198,7 +199,7 @@ def tile_picked_hop2_relu_e_kernel(
                     lhsT=words.bitcast(FP8X4),
                     lhsT_scale=scales,
                     rhs=moving.bitcast(FP8X4),
-                    rhs_scale=picked_scales[4 * g : P, f : f + c],
+                    rhs_scale=picked_scales[4 - 4 * g : P, f : f + c],
                     start=(g == 0),
                     stop=(g == PASSES - 1 and f + c == first + count),
                 )
@@ -241,9 +242,7 @@ def tile_picked_hop2_relu_e_kernel(
         sums = {(0, b): first_sums[:, b] for b in range(2)}
         for (u, b), bank in {(0, 2): 0, (1, 0): 7, (1, 1): 2, (1, 2): 1}.items():
             sums[(u, b)] = psum.tile([P, 2, P], F32, name=f"sums{u}_{b}", tag=f"bank{bank}")[:]
-        back01 = psum.tile([P, 2, 2, P], F32, name="back01", tag="bank5")
-        back2 = psum.tile([P, 2, P], F32, name="back2", tag="bank6")
-        back = [back01[:, 0], back01[:, 1], back2[:]]
+        back = [psum.tile([P, 2, P], F32, name=f"back{b}", tag=f"bank{bank}") for b, bank in enumerate((5, 6, 3))]
 
         def turn(t, b, d):
             nc.tensor.matmul(
@@ -277,10 +276,9 @@ def tile_picked_hop2_relu_e_kernel(
 
         z01 = keep.tile([P, 2 * P, PACK], BF16, name="z01", align_bytes=ALIGN)
         z2 = keep.tile([P, P, PACK], BF16, name="z2", align_bytes=ALIGN)
-        pairs = z01[:].rearrange("p v t -> p (v t)").bitcast(F32).rearrange("p (b v u) -> p b v u", b=2, u=2)
-        nc.scalar.copy(pairs, back01[:].rearrange("p b u v -> p b v u"))
-        pairs = z2[:].rearrange("p v t -> p (v t)").bitcast(F32).rearrange("p (v u) -> p v u", u=2)
-        nc.scalar.copy(pairs, back2[:].rearrange("p u v -> p v u"))
+        for b, block in enumerate((z01[:, :P], z01[:, P:], z2[:])):
+            pairs = block.rearrange("p v t -> p (v t)").bitcast(F32).rearrange("p (v u) -> p v u", u=2)
+            nc.scalar.copy(pairs, back[b][:].rearrange("p u v -> p v u"))
 
         z_codes = []
         for n, (v0, width) in enumerate(Z_GROUPS):

@@ -41,9 +41,9 @@ W_LOADS = [(0, 0, 256, "w_first"), (0, 256, 256, "w_raw0"), (1, 0, 384, "w_third
 TWO_STRETCHES = [(0, BANK), (BANK, BANK)]
 THREE_STRETCHES = [(0, BANK), (BANK, BANK // 2), (BANK + BANK // 2, BANK // 2)]
 HEAD = 3 * BANK // 2
-STRETCHES = [THREE_STRETCHES, TWO_STRETCHES, TWO_STRETCHES, THREE_STRETCHES]
+STRETCHES = [THREE_STRETCHES, TWO_STRETCHES, TWO_STRETCHES, TWO_STRETCHES]
 EARLY_BANKS = {(0, 0): 0, (0, 1): 1, (0, 2): 2, (1, 0): 3, (1, 1): 4}
-LATE_BANKS = {(2, 0): 0, (3, 0): 1, (3, 1): 3, (2, 1): 4, (3, 2): 0}
+LATE_BANKS = {(2, 0): 0, (2, 1): 1, (3, 0): 3, (3, 1): 4}
 
 Z_GROUPS = [(0, 2 * P), (2 * P, P), (3 * P, P)]
 TURNED_BLOCKS = 3
@@ -176,7 +176,7 @@ def tile_picked_hop2_relu_e_kernel(
         late_keys = [(g, t) for g in range(PASSES) for t in (2, 3)]
         quantise_w("late", late[:].rearrange("p g e m j -> p (g e m j)"), late_keys)
 
-        terms = [keep.tile([P, PACK, V], F32, name=f"terms{d}") for d in range(HOPS)]
+        terms = [keep.tile([P, PACK, TURNED_BLOCKS * P], F32, name=f"terms{d}") for d in range(HOPS)]
         h_rows = [keep.tile([P, S], F32, name=f"h{t}") for t in range(PACK)]
         bank_of = EARLY_BANKS | LATE_BANKS
         groups = {}
@@ -212,9 +212,9 @@ def tile_picked_hop2_relu_e_kernel(
             else:
                 nc.scalar.activation(dst, groups[(t, n)][:, :count], RELU)
 
-        def weigh(t, d, v0, width):
+        def weigh(t, d, v0, width, dst=None):
             nc.vector.tensor_tensor(
-                terms[d][:, t, v0 : v0 + width],
+                terms[d][:, t, v0 : v0 + width] if dst is None else dst,
                 h_rows[t][:].indirect(entries(pos_t[d], v0, width)),
                 gate_t[d][:, v0 : v0 + width],
                 MULT,
@@ -228,19 +228,19 @@ def tile_picked_hop2_relu_e_kernel(
             for n in range(len(STRETCHES[t])):
                 leave_bank(t, n)
             for d in range(HOPS):
-                weigh(t, d, 0, V)
+                weigh(t, d, 0, TURNED_BLOCKS * P)
         for t, n in LATE_BANKS:
             for g in range(PASSES):
                 multiply(t, g, n)
             leave_bank(t, n)
-        for v0, width in Z_GROUPS:
-            for t in (2, 3):
-                for d in range(HOPS):
-                    weigh(t, d, v0, width)
+        for t, d in ((2, 0), (2, 1), (3, 0)):
+            weigh(t, d, 0, TURNED_BLOCKS * P)
+        for v0, width in Z_GROUPS[:2]:
+            weigh(3, 1, v0, width)
 
         first_sums = psum.tile([P, 2, 2, P], F32, name="first_sums", tag="bank4")
         sums = {(0, b): first_sums[:, b] for b in range(2)}
-        for (u, b), bank in {(0, 2): 0, (1, 0): 7, (1, 1): 2, (1, 2): 1}.items():
+        for (u, b), bank in {(0, 2): 3, (1, 0): 7, (1, 1): 2, (1, 2): 1}.items():
             sums[(u, b)] = psum.tile([P, 2, P], F32, name=f"sums{u}_{b}", tag=f"bank{bank}")[:]
         back = [psum.tile([P, 2, P], F32, name=f"back{b}", tag=f"bank{bank}") for b, bank in enumerate((5, 6, 3))]
 
@@ -255,7 +255,7 @@ def tile_picked_hop2_relu_e_kernel(
             )
 
         def round_and_turn_back(u, b):
-            tile = keep.tile([P, P, 2], BF16, name=f"turned{u}_{b}", align_bytes=ALIGN)
+            tile = keep.tile([P, P, 2], BF16, name=f"turned{u}_{b}", tag=f"turned{u}_{b}", align_bytes=ALIGN)
             nc.scalar.copy(tile[:], sums[(u, b)].rearrange("v e m -> v m e"))
             words = tile[:].rearrange("v m e -> v (m e)").bitcast(F32)
             nc.tensor.transpose(back[b][:, u, :], words, identity[:])
@@ -273,6 +273,14 @@ def tile_picked_hop2_relu_e_kernel(
                         turn(t, b, d)
             for b in blocks:
                 round_and_turn_back(1, b)
+
+        last_terms = [
+            keep.tile([P, PACK, P], F32, name=f"last_terms{d}", tag=f"turned0_{d}", align_bytes=ALIGN)
+            for d in range(HOPS)
+        ]
+        for t in range(PACK):
+            for d in range(HOPS):
+                weigh(t, d, TURNED_BLOCKS * P, P, last_terms[d][:, t, :])
 
         z01 = keep.tile([P, 2 * P, PACK], BF16, name="z01", align_bytes=ALIGN)
         z2 = keep.tile([P, P, PACK], BF16, name="z2", align_bytes=ALIGN)
@@ -296,7 +304,7 @@ def tile_picked_hop2_relu_e_kernel(
 
         quantise_z(0, 0, z01[:, :P])
         quantise_z(0, P, z01[:, P:])
-        views = [terms[d][:, :, 3 * P :].rearrange("p t (c i) -> p c t i", i=2) for d in range(HOPS)]
+        views = [last_terms[d][:].rearrange("p t (c i) -> p c t i", i=2) for d in range(HOPS)]
         nc.vector.tensor_tensor(z01[:, :P].rearrange("p (c i) t -> p c t i", i=2), views[0], views[1], ADD)
         quantise_z(1, 0, z2[:])
         quantise_z(2, 0, z01[:, :P])

@@ -153,8 +153,8 @@ def tile_picked_hop2_relu_e_kernel(
 
         stationary = {}
 
-        def quantise_w(name, source, keys):
-            words = keep.tile([P, len(keys) * P], U32, name=f"w_words_{name}", align_bytes=ALIGN)
+        def quantise_w(name, source, keys, tag=None):
+            words = keep.tile([P, len(keys) * P], U32, name=f"w_words_{name}", tag=tag or name, align_bytes=ALIGN)
             scales = keep.tile([P, len(keys) * P], U8, name=f"w_scales_{name}", align_bytes=ALIGN)
             nc.vector.quantize_mx(out=words[:].bitcast(FP8X4), scales=scales[:], in_=source)
             for n, key in enumerate(keys):
@@ -167,14 +167,16 @@ def tile_picked_hop2_relu_e_kernel(
         nc.vector.tensor_copy(picked_scales[:], x_scales[:].indirect(offs_t[:]))
         quantise_early(0)
         head = keep.tile([P, HEAD], U32, name="picked1_head", tag="w_raw0", align_bytes=ALIGN)
-        for first, count in THREE_STRETCHES[:2]:
-            nc.vector.tensor_copy(head[:, first : first + count], x_words[1][:].indirect(entries(offs_t, first, count)))
+        nc.vector.tensor_copy(head[:], x_words[1][:].indirect(entries(offs_t, 0, HEAD)))
         quantise_early(1)
         first, count = THREE_STRETCHES[2]
         tail = keep.tile([P, count], U32, name="picked1_tail", tag="w_last", align_bytes=ALIGN)
         nc.vector.tensor_copy(tail[:], x_words[1][:].indirect(entries(offs_t, first, count)))
-        late_keys = [(g, t) for g in range(PASSES) for t in (2, 3)]
-        quantise_w("late", late[:].rearrange("p g e m j -> p (g e m j)"), late_keys)
+
+        def quantise_late(g, tag=None):
+            quantise_w(f"late{g}", late[:, g].rearrange("p e m j -> p (e m j)"), [(g, 2), (g, 3)], tag)
+
+        quantise_late(0, "w_third")
 
         terms = [keep.tile([P, PACK, TURNED_BLOCKS * P], F32, name=f"terms{d}") for d in range(HOPS)]
         h_rows = [keep.tile([P, S], F32, name=f"h{t}") for t in range(PACK)]
@@ -227,6 +229,8 @@ def tile_picked_hop2_relu_e_kernel(
                 multiply(t, 1, n)
             for n in range(len(STRETCHES[t])):
                 leave_bank(t, n)
+            if t == 0:
+                quantise_late(1)
             for d in range(HOPS):
                 weigh(t, d, 0, TURNED_BLOCKS * P)
         for t, n in LATE_BANKS:

@@ -40,6 +40,7 @@ W_LOADS = [(0, 0, 256, "w_first"), (0, 256, 256, "w_raw0"), (1, 0, 384, "w_third
 
 TWO_STRETCHES = [(0, BANK), (BANK, BANK)]
 THREE_STRETCHES = [(0, BANK), (BANK, BANK // 2), (BANK + BANK // 2, BANK // 2)]
+WARM_UPS = 2
 HEAD = 3 * BANK // 2
 STRETCHES = [THREE_STRETCHES, TWO_STRETCHES, TWO_STRETCHES, TWO_STRETCHES]
 EARLY_BANKS = {(0, 0): 0, (0, 1): 1, (0, 2): 2, (1, 0): 3, (1, 1): 4}
@@ -164,7 +165,21 @@ def tile_picked_hop2_relu_e_kernel(
             quantise_w(f"early{g}", early[g][:].rearrange("p e m j -> p (e m j)"), [(g, 0), (g, 1)])
 
         picked_scales = keep.tile([P, S], U8, name="picked_scales", align_bytes=ALIGN)
-        nc.vector.tensor_copy(picked_scales[:], x_scales[:].indirect(offs_t[:]))
+        for first, count in TWO_STRETCHES:
+            nc.vector.tensor_copy(
+                picked_scales[:, first : first + count], x_scales[:].indirect(entries(offs_t, first, count))
+            )
+        warm = psum.tile([P, BANK], F32, name="warm", tag="bank7")
+        for n in range(WARM_UPS):
+            nc.tensor.matmul_mx(
+                out=warm[:],
+                lhsT=picked0[:, :P].bitcast(FP8X4),
+                lhsT_scale=picked_scales[4:P, :P],
+                rhs=picked0[:, :BANK].bitcast(FP8X4),
+                rhs_scale=picked_scales[4:P, :BANK],
+                start=True,
+                stop=True,
+            )
         quantise_early(0)
         head = keep.tile([P, HEAD], U32, name="picked1_head", tag="w_raw0", align_bytes=ALIGN)
         nc.vector.tensor_copy(head[:], x_words[1][:].indirect(entries(offs_t, 0, HEAD)))

@@ -42,8 +42,9 @@ TWO_STRETCHES = [(0, BANK), (BANK, BANK)]
 THREE_STRETCHES = [(0, BANK), (BANK, BANK // 2), (BANK + BANK // 2, BANK // 2)]
 WARM_UPS = 2
 HEAD = 3 * BANK // 2
-STRETCHES = [THREE_STRETCHES, TWO_STRETCHES, TWO_STRETCHES, TWO_STRETCHES]
-EARLY_BANKS = {(0, 0): 0, (0, 1): 1, (0, 2): 2, (1, 0): 3, (1, 1): 4}
+FOUR_STRETCHES = [(n * BANK // 2, BANK // 2) for n in range(4)]
+STRETCHES = [FOUR_STRETCHES, TWO_STRETCHES, TWO_STRETCHES, TWO_STRETCHES]
+EARLY_BANKS = {(0, 0): 0, (0, 1): 1, (0, 2): 2, (0, 3): 5, (1, 0): 3, (1, 1): 4}
 LATE_BANKS = {(2, 0): 0, (2, 1): 1, (3, 0): 3, (3, 1): 4}
 
 Z_GROUPS = [(0, 2 * P), (2 * P, P), (3 * P, P)]
@@ -58,6 +59,7 @@ def tile_picked_hop2_relu_e_kernel(
     with ExitStack() as ctx:
         lists = ctx.enter_context(tc.tile_pool(name="lists", bufs=1))
         keep = ctx.enter_context(tc.tile_pool(name="keep", bufs=1))
+        shared = ctx.enter_context(tc.tile_pool(name="shared", bufs=1))
         psum = ctx.enter_context(tc.psum_pool(name="psum", bufs=1))
 
         def load_list(src, name):
@@ -90,7 +92,10 @@ def tile_picked_hop2_relu_e_kernel(
                 offs_t = load_list(offs, "offs_t")
         w_raw = []
         for g, c0, width, tag in W_LOADS:
-            raw = keep.tile([P, PACK, width], F32, name=f"w_raw{g}_{c0}", tag=tag, align_bytes=ALIGN)
+            if tag == "w_last":
+                raw = shared.tile([P, PACK, width], F32, name="w_last", offset=0, align_bytes=ALIGN)
+            else:
+                raw = keep.tile([P, PACK, width], F32, name=f"w_raw{g}_{c0}", tag=tag, align_bytes=ALIGN)
             nc.sync.dma_start(raw[:], pass_rows(w1, g)[:, :, c0 : c0 + width])
             w_raw.append((g, c0, width, raw))
         pos_t, gate_t = [], []
@@ -134,15 +139,12 @@ def tile_picked_hop2_relu_e_kernel(
             if (g, c0) == (1, 0):
                 nc.vector.tensor_copy(picked0[:], x_words[0][:].indirect(offs_t[:]))
 
-        early = [
-            keep.tile([P, 2, P, PACK], BF16, name=f"w_early{g}", tag=f"w_early{g}", align_bytes=ALIGN)
-            for g in range(PASSES)
-        ]
+        early = keep.tile([P, 2, PASSES, P, PACK], BF16, name="w_early", align_bytes=ALIGN)
         late = keep.tile([P, PASSES, 2, P, PACK], BF16, name="w_late", align_bytes=ALIGN)
 
         def deal(load, u):
             g, c0, width, raw = w_raw[load]
-            tile = early[g][:] if u == 0 else late[:, g]
+            tile = early[:, :, g] if u == 0 else late[:, g]
             dst = tile.rearrange("p e m j -> p m j e")[:, c0 // PACK : (c0 + width) // PACK]
             src = raw[:].rearrange("p j (m t) -> p m j t", t=PACK)[:, :, :, 2 * u : 2 * u + 2]
             nc.scalar.copy(dst, src)
@@ -154,15 +156,16 @@ def tile_picked_hop2_relu_e_kernel(
 
         stationary = {}
 
-        def quantise_w(name, source, keys, tag=None):
-            words = keep.tile([P, len(keys) * P], U32, name=f"w_words_{name}", tag=tag or name, align_bytes=ALIGN)
+        def quantise_w(name, source, keys, tag=None, words=None):
+            if words is None:
+                words = keep.tile([P, len(keys) * P], U32, name=f"w_words_{name}", tag=tag or name, align_bytes=ALIGN)
             scales = keep.tile([P, len(keys) * P], U8, name=f"w_scales_{name}", align_bytes=ALIGN)
             nc.vector.quantize_mx(out=words[:].bitcast(FP8X4), scales=scales[:], in_=source)
             for n, key in enumerate(keys):
                 stationary[key] = (words[:, n * P : (n + 1) * P], scales[:, n * P : (n + 1) * P])
 
         def quantise_early(g):
-            quantise_w(f"early{g}", early[g][:].rearrange("p e m j -> p (e m j)"), [(g, 0), (g, 1)])
+            quantise_w(f"early{g}", early[:, 0, g].rearrange("p m j -> p (m j)"), [(g, 0)])
 
         picked_scales = keep.tile([P, S], U8, name="picked_scales", align_bytes=ALIGN)
         for first, count in TWO_STRETCHES:
@@ -185,15 +188,23 @@ def tile_picked_hop2_relu_e_kernel(
         nc.vector.tensor_copy(head[:], x_words[1][:].indirect(entries(offs_t, 0, HEAD)))
         quantise_early(1)
         first, count = THREE_STRETCHES[2]
-        tail = keep.tile([P, count], U32, name="picked1_tail", tag="w_last", align_bytes=ALIGN)
+        tail = shared.tile([P, count], U32, name="picked1_tail", offset=0, align_bytes=ALIGN)
         nc.vector.tensor_copy(tail[:], x_words[1][:].indirect(entries(offs_t, first, count)))
+        second = shared.tile([P, PASSES * P], U32, name="w_words_second", offset=4 * count, align_bytes=ALIGN)
+        quantise_w("second", early[:, 1].rearrange("p g m j -> p (g m j)"), [(0, 1), (1, 1)], words=second)
 
         def quantise_late(g, tag=None):
             quantise_w(f"late{g}", late[:, g].rearrange("p e m j -> p (e m j)"), [(g, 2), (g, 3)], tag)
 
         quantise_late(0, "w_third")
 
-        terms = [keep.tile([P, PACK, TURNED_BLOCKS * P], F32, name=f"terms{d}") for d in range(HOPS)]
+        wide = TURNED_BLOCKS * P
+        rows = [keep.tile([P, PACK * V], F32, name=f"terms{d}", align_bytes=ALIGN) for d in range(HOPS)]
+
+        def term(t, d, v0, width):
+            first = (t - 1) % PACK * wide + v0 if v0 < wide else PACK * wide + t * P
+            return rows[d][:, first : first + width]
+
         h_rows = [keep.tile([P, S], F32, name=f"h{t}") for t in range(PACK)]
         bank_of = EARLY_BANKS | LATE_BANKS
         groups = {}
@@ -204,11 +215,10 @@ def tile_picked_hop2_relu_e_kernel(
                 groups[(t, n)] = psum.tile([P, BANK], F32, name=f"h_bank{t}_{n}", tag=f"bank{bank_of[(t, n)]}")
                 pieces = [(first, count, picked0[:, first : first + count])]
             else:
-                pieces = [
-                    (f, c, head[:, f : f + c] if f + c <= HEAD else tail[:])
-                    for f, c in THREE_STRETCHES
-                    if first <= f < first + count
-                ]
+                in_head = min(count, HEAD - first)
+                pieces = [(first, in_head, head[:, first : first + in_head])] if in_head > 0 else []
+                if first + count > HEAD:
+                    pieces.append((HEAD, S - HEAD, tail[:]))
             words, scales = stationary[(g, t)]
             for f, c, moving in pieces:
                 nc.tensor.matmul_mx(
@@ -224,38 +234,41 @@ def tile_picked_hop2_relu_e_kernel(
         def leave_bank(t, n):
             first, count = STRETCHES[t][n]
             dst = h_rows[t][:, first : first + count]
-            if (t, n) == (0, 1):
+            if (t, n) == (0, 2):
                 nc.vector.tensor_scalar_max(dst, groups[(t, n)][:, :count], 0.0)
             else:
                 nc.scalar.activation(dst, groups[(t, n)][:, :count], RELU)
 
-        def weigh(t, d, v0, width, dst=None):
+        def weigh(t, d, v0, width):
             nc.vector.tensor_tensor(
-                terms[d][:, t, v0 : v0 + width] if dst is None else dst,
+                term(t, d, v0, width),
                 h_rows[t][:].indirect(entries(pos_t[d], v0, width)),
                 gate_t[d][:, v0 : v0 + width],
                 MULT,
             )
 
-        for t, n in EARLY_BANKS:
-            multiply(t, 0, n)
+        for n in range(len(STRETCHES[0])):
+            multiply(0, 0, n)
         for t in (0, 1):
             for n in range(len(STRETCHES[t])):
+                if t == 1:
+                    multiply(t, 0, n)
                 multiply(t, 1, n)
             for n in range(len(STRETCHES[t])):
                 leave_bank(t, n)
             if t == 0:
                 quantise_late(1)
             for d in range(HOPS):
-                weigh(t, d, 0, TURNED_BLOCKS * P)
+                weigh(t, d, 0, V if t == 0 else wide)
         for t, n in LATE_BANKS:
             for g in range(PASSES):
                 multiply(t, g, n)
             leave_bank(t, n)
-        for t, d in ((2, 0), (2, 1), (3, 0)):
-            weigh(t, d, 0, TURNED_BLOCKS * P)
+        for d in range(HOPS):
+            weigh(2, d, 0, TURNED_BLOCKS * P)
         for v0, width in Z_GROUPS[:2]:
-            weigh(3, 1, v0, width)
+            for d in range(HOPS):
+                weigh(3, d, v0, width)
 
         first_sums = psum.tile([P, 2, 2, P], F32, name="first_sums", tag="bank4")
         sums = {(0, b): first_sums[:, b] for b in range(2)}
@@ -266,7 +279,7 @@ def tile_picked_hop2_relu_e_kernel(
         def turn(t, b, d):
             nc.tensor.matmul(
                 sums[(t // 2, b)][:, t % 2, :],
-                lhsT=terms[d][:, t, b * P : (b + 1) * P],
+                lhsT=term(t, d, b * P, P),
                 rhs=identity[:],
                 start=(d == 0),
                 stop=(d == HOPS - 1),
@@ -274,9 +287,13 @@ def tile_picked_hop2_relu_e_kernel(
             )
 
         def round_and_turn_back(u, b):
-            tile = keep.tile([P, P, 2], BF16, name=f"turned{u}_{b}", tag=f"turned{u}_{b}", align_bytes=ALIGN)
-            nc.scalar.copy(tile[:], sums[(u, b)].rearrange("v e m -> v m e"))
-            words = tile[:].rearrange("v m e -> v (m e)").bitcast(F32)
+            if u == 0 and b < HOPS:
+                first = PACK * wide + P + P // 2
+                words = rows[b][:, first : first + P]
+            else:
+                words = keep.tile([P, P], F32, name=f"turned{u}_{b}", align_bytes=ALIGN)[:]
+            pairs = words.bitcast(BF16).rearrange("v (m e) -> v m e", e=2)
+            nc.scalar.copy(pairs, sums[(u, b)].rearrange("v e m -> v m e"))
             nc.tensor.transpose(back[b][:, u, :], words, identity[:])
 
         for t in (0, 1):
@@ -293,13 +310,9 @@ def tile_picked_hop2_relu_e_kernel(
             for b in blocks:
                 round_and_turn_back(1, b)
 
-        last_terms = [
-            keep.tile([P, PACK, P], F32, name=f"last_terms{d}", tag=f"turned0_{d}", align_bytes=ALIGN)
-            for d in range(HOPS)
-        ]
-        for t in range(PACK):
+        for t in range(1, PACK):
             for d in range(HOPS):
-                weigh(t, d, TURNED_BLOCKS * P, P, last_terms[d][:, t, :])
+                weigh(t, d, wide, P)
 
         z01 = keep.tile([P, 2 * P, PACK], BF16, name="z01", align_bytes=ALIGN)
         z2 = keep.tile([P, P, PACK], BF16, name="z2", align_bytes=ALIGN)
@@ -323,7 +336,7 @@ def tile_picked_hop2_relu_e_kernel(
 
         quantise_z(0, 0, z01[:, :P])
         quantise_z(0, P, z01[:, P:])
-        views = [last_terms[d][:].rearrange("p t (c i) -> p c t i", i=2) for d in range(HOPS)]
+        views = [rows[d][:, PACK * wide :].rearrange("p (t c i) -> p c t i", t=PACK, i=2) for d in range(HOPS)]
         nc.vector.tensor_tensor(z01[:, :P].rearrange("p (c i) t -> p c t i", i=2), views[0], views[1], ADD)
         quantise_z(1, 0, z2[:])
         quantise_z(2, 0, z01[:, :P])

@@ -147,7 +147,11 @@ def tile_picked_hop2_relu_e_kernel(
             tile = early[:, :, g] if u == 0 else late[:, g]
             dst = tile.rearrange("p e m j -> p m j e")[:, c0 // PACK : (c0 + width) // PACK]
             src = raw[:].rearrange("p j (m t) -> p m j t", t=PACK)[:, :, :, 2 * u : 2 * u + 2]
-            nc.scalar.copy(dst, src)
+            if u == 1 and load < len(W_LOADS) - 1:
+                order = "p m j e -> p m e j"
+                nc.gpsimd.tensor_scalar(dst.rearrange(order), src.rearrange(order), 1.0, 0.0, MULT, ADD)
+            else:
+                nc.scalar.copy(dst, src)
 
         for load in range(len(W_LOADS)):
             deal(load, 0)
@@ -156,10 +160,12 @@ def tile_picked_hop2_relu_e_kernel(
 
         stationary = {}
 
-        def quantise_w(name, source, keys, tag=None, words=None):
-            if words is None:
-                words = keep.tile([P, len(keys) * P], U32, name=f"w_words_{name}", tag=tag or name, align_bytes=ALIGN)
-            scales = keep.tile([P, len(keys) * P], U8, name=f"w_scales_{name}", align_bytes=ALIGN)
+        def quantise_w(name, source, keys, offset=None):
+            words = keep.tile([P, len(keys) * P], U32, name=f"w_words_{name}", align_bytes=ALIGN)
+            if offset is None:
+                scales = keep.tile([P, len(keys) * P], U8, name=f"w_scales_{name}", align_bytes=ALIGN)
+            else:
+                scales = shared.tile([P, len(keys) * P], U8, name=f"w_scales_{name}", offset=offset, align_bytes=ALIGN)
             nc.vector.quantize_mx(out=words[:].bitcast(FP8X4), scales=scales[:], in_=source)
             for n, key in enumerate(keys):
                 stationary[key] = (words[:, n * P : (n + 1) * P], scales[:, n * P : (n + 1) * P])
@@ -190,13 +196,12 @@ def tile_picked_hop2_relu_e_kernel(
         first, count = THREE_STRETCHES[2]
         tail = shared.tile([P, count], U32, name="picked1_tail", offset=0, align_bytes=ALIGN)
         nc.vector.tensor_copy(tail[:], x_words[1][:].indirect(entries(offs_t, first, count)))
-        second = shared.tile([P, PASSES * P], U32, name="w_words_second", offset=4 * count, align_bytes=ALIGN)
-        quantise_w("second", early[:, 1].rearrange("p g m j -> p (g m j)"), [(0, 1), (1, 1)], words=second)
+        quantise_w("second", early[:, 1].rearrange("p g m j -> p (g m j)"), [(0, 1), (1, 1)], 4 * count)
 
-        def quantise_late(g, tag=None):
-            quantise_w(f"late{g}", late[:, g].rearrange("p e m j -> p (e m j)"), [(g, 2), (g, 3)], tag)
+        def quantise_late(g, offset=None):
+            quantise_w(f"late{g}", late[:, g].rearrange("p e m j -> p (e m j)"), [(g, 2), (g, 3)], offset)
 
-        quantise_late(0, "w_third")
+        quantise_late(0, 4 * count + 2 * P)
 
         wide = TURNED_BLOCKS * P
         rows = [keep.tile([P, PACK * V], F32, name=f"terms{d}", align_bytes=ALIGN) for d in range(HOPS)]
@@ -234,7 +239,7 @@ def tile_picked_hop2_relu_e_kernel(
         def leave_bank(t, n):
             first, count = STRETCHES[t][n]
             dst = h_rows[t][:, first : first + count]
-            if (t, n) == (0, 2):
+            if (t, n) == (0, 0):
                 nc.vector.tensor_scalar_max(dst, groups[(t, n)][:, :count], 0.0)
             else:
                 nc.scalar.activation(dst, groups[(t, n)][:, :count], RELU)

@@ -142,21 +142,26 @@ def tile_picked_hop2_relu_e_kernel(
         early = keep.tile([P, 2, PASSES, P, PACK], BF16, name="w_early", align_bytes=ALIGN)
         late = keep.tile([P, PASSES, 2, P, PACK], BF16, name="w_late", align_bytes=ALIGN)
 
-        def deal(load, u):
+        def deal(load, u, on_gpsimd, part=slice(None)):
             g, c0, width, raw = w_raw[load]
             tile = early[:, :, g] if u == 0 else late[:, g]
             dst = tile.rearrange("p e m j -> p m j e")[:, c0 // PACK : (c0 + width) // PACK]
             src = raw[:].rearrange("p j (m t) -> p m j t", t=PACK)[:, :, :, 2 * u : 2 * u + 2]
-            if u == 1 and load < len(W_LOADS) - 1:
+            dst, src = dst[:, part], src[:, part]
+            if on_gpsimd:
                 order = "p m j e -> p m e j"
                 nc.gpsimd.tensor_scalar(dst.rearrange(order), src.rearrange(order), 1.0, 0.0, MULT, ADD)
             else:
                 nc.scalar.copy(dst, src)
 
-        for load in range(len(W_LOADS)):
-            deal(load, 0)
-        for load in (0, 1, 3, 2):
-            deal(load, 1)
+        for load in (0, 1):
+            deal(load, 0, False)
+            deal(load, 1, True)
+        deal(2, 0, False, slice(0, 80))
+        deal(2, 0, True, slice(80, 96))
+        deal(3, 0, False)
+        deal(3, 1, True)
+        deal(2, 1, False)
 
         stationary = {}
 

@@ -42,14 +42,14 @@ TWO_STRETCHES = [(0, BANK), (BANK, BANK)]
 THREE_STRETCHES = [(0, BANK), (BANK, BANK // 2), (BANK + BANK // 2, BANK // 2)]
 WARM_UPS = 2
 HEAD = 3 * BANK // 2
-FOUR_STRETCHES = [(n * BANK // 2, BANK // 2) for n in range(4)]
+FOUR_STRETCHES = [(0, P), (P, 2 * P), (3 * P, 3 * P), (HEAD, S - HEAD)]
 STRETCHES = [FOUR_STRETCHES, TWO_STRETCHES, TWO_STRETCHES, TWO_STRETCHES]
 EARLY_BANKS = {(0, 0): 0, (0, 1): 1, (0, 2): 2, (0, 3): 5, (1, 0): 3, (1, 1): 4}
 LATE_BANKS = {(2, 0): 0, (2, 1): 1, (3, 0): 3, (3, 1): 4}
 
 Z_GROUPS = [(0, 2 * P), (2 * P, P), (3 * P, P)]
 TURNED_BLOCKS = 3
-G_BANKS = [(4, 0), (7, 2), (5, 1)]
+G_BANKS = [(1, 0), (7, 2), (5, 4)]
 
 
 def tile_picked_hop2_relu_e_kernel(
@@ -139,7 +139,7 @@ def tile_picked_hop2_relu_e_kernel(
             if (g, c0) == (1, 0):
                 nc.vector.tensor_copy(picked0[:], x_words[0][:].indirect(offs_t[:]))
 
-        early = keep.tile([P, 2, PASSES, P, PACK], BF16, name="w_early", align_bytes=ALIGN)
+        early = keep.tile([P, 2, PASSES, P, PACK], BF16, name="w_early", tag="w_early", align_bytes=ALIGN)
         late = keep.tile([P, PASSES, 2, P, PACK], BF16, name="w_late", align_bytes=ALIGN)
 
         def deal(load, u, on_gpsimd, part=slice(None)):
@@ -165,8 +165,8 @@ def tile_picked_hop2_relu_e_kernel(
 
         stationary = {}
 
-        def quantise_w(name, source, keys, offset=None):
-            words = keep.tile([P, len(keys) * P], U32, name=f"w_words_{name}", align_bytes=ALIGN)
+        def quantise_w(name, source, keys, offset=None, tag=None):
+            words = keep.tile([P, len(keys) * P], U32, name=f"w_words_{name}", tag=tag or name, align_bytes=ALIGN)
             if offset is None:
                 scales = keep.tile([P, len(keys) * P], U8, name=f"w_scales_{name}", align_bytes=ALIGN)
             else:
@@ -203,11 +203,6 @@ def tile_picked_hop2_relu_e_kernel(
         nc.vector.tensor_copy(tail[:], x_words[1][:].indirect(entries(offs_t, first, count)))
         quantise_w("second", early[:, 1].rearrange("p g m j -> p (g m j)"), [(0, 1), (1, 1)], 4 * count)
 
-        def quantise_late(g, offset=None):
-            quantise_w(f"late{g}", late[:, g].rearrange("p e m j -> p (e m j)"), [(g, 2), (g, 3)], offset)
-
-        quantise_late(0, 4 * count + 2 * P)
-
         wide = TURNED_BLOCKS * P
         rows = [keep.tile([P, PACK * V], F32, name=f"terms{d}", align_bytes=ALIGN) for d in range(HOPS)]
 
@@ -224,9 +219,13 @@ def tile_picked_hop2_relu_e_kernel(
             if g == 0:
                 groups[(t, n)] = psum.tile([P, BANK], F32, name=f"h_bank{t}_{n}", tag=f"bank{bank_of[(t, n)]}")
                 pieces = [(first, count, picked0[:, first : first + count])]
+                if count == 3 * P:
+                    pieces = [(f, c, picked0[:, f : f + c]) for f, c in ((first, 2 * P), (first + 2 * P, P))]
             else:
                 in_head = min(count, HEAD - first)
                 pieces = [(first, in_head, head[:, first : first + in_head])] if in_head > 0 else []
+                if count == 3 * P:
+                    pieces = [(f, c, head[:, f : f + c]) for f, c in ((first, 2 * P), (first + 2 * P, P))]
                 if first + count > HEAD:
                     pieces.append((HEAD, S - HEAD, tail[:]))
             words, scales = stationary[(g, t)]
@@ -237,7 +236,7 @@ def tile_picked_hop2_relu_e_kernel(
                     lhsT_scale=scales,
                     rhs=moving.bitcast(FP8X4),
                     rhs_scale=picked_scales[4 - 4 * g : P, f : f + c],
-                    start=(g == 0),
+                    start=(g == 0 and f == first),
                     stop=(g == PASSES - 1 and f + c == first + count),
                 )
 
@@ -267,7 +266,8 @@ def tile_picked_hop2_relu_e_kernel(
             for n in range(len(STRETCHES[t])):
                 leave_bank(t, n)
             if t == 0:
-                quantise_late(1)
+                keys = [(g, late_tile) for g in range(PASSES) for late_tile in (2, 3)]
+                quantise_w("late", late[:].rearrange("p g e m j -> p (g e m j)"), keys, tag="w_early")
             for d in range(HOPS):
                 weigh(t, d, 0, V if t == 0 else wide)
         for t, n in LATE_BANKS:
@@ -280,9 +280,9 @@ def tile_picked_hop2_relu_e_kernel(
             for d in range(HOPS):
                 weigh(3, d, v0, width)
 
-        first_sums = psum.tile([P, 2, 2, P], F32, name="first_sums", tag="bank4")
+        first_sums = psum.tile([P, 2, 2, P], F32, name="first_sums", tag="bank1")
         sums = {(0, b): first_sums[:, b] for b in range(2)}
-        for (u, b), bank in {(0, 2): 3, (1, 0): 7, (1, 1): 2, (1, 2): 1}.items():
+        for (u, b), bank in {(0, 2): 0, (1, 0): 7, (1, 1): 2, (1, 2): 4}.items():
             sums[(u, b)] = psum.tile([P, 2, P], F32, name=f"sums{u}_{b}", tag=f"bank{bank}")[:]
         back = [psum.tile([P, 2, P], F32, name=f"back{b}", tag=f"bank{bank}") for b, bank in enumerate((5, 6, 3))]
 

@@ -49,7 +49,7 @@ LATE_BANKS = {(2, 0): 0, (2, 1): 1, (3, 0): 3, (3, 1): 4}
 
 Z_GROUPS = [(0, 2 * P), (2 * P, P), (3 * P, P)]
 TURNED_BLOCKS = 3
-G_BANKS = [(1, 0), (7, 2), (5, 4)]
+G_BANKS = [1, 2, 7, 0]
 
 
 def tile_picked_hop2_relu_e_kernel(
@@ -352,12 +352,13 @@ def tile_picked_hop2_relu_e_kernel(
         quantise_z(2, 0, z01[:, :P])
 
         g_rows = [keep.tile([P, V], F32, name=f"g_rows{m}") for m in range(N // P)]
+        second_rows = psum.tile([P, V], F32, name="second_rows", tag=f"bank{G_BANKS[-1]}")
         for n, (v0, width) in enumerate(Z_GROUPS):
-            for m in range(N // P):
-                bank = psum.tile([P, BANK], F32, name=f"g_bank{n}_{m}", tag=f"bank{G_BANKS[n][m]}")
-                z_words, z_scales = z_codes[n]
+            first_rows = psum.tile([P, BANK], F32, name=f"first_rows{n}", tag=f"bank{G_BANKS[n]}")
+            z_words, z_scales = z_codes[n]
+            for m, dst in enumerate((first_rows[:, :width], second_rows[:, v0 : v0 + width])):
                 nc.tensor.matmul_mx(
-                    out=bank[:, :width],
+                    out=dst,
                     lhsT=w2_codes[:, 2 * P * m : 2 * P * (m + 1)].bitcast(FP4X4),
                     lhsT_scale=w2_plane[:, P * m : P * (m + 1)],
                     rhs=z_words[:].bitcast(FP8X4),
@@ -365,8 +366,8 @@ def tile_picked_hop2_relu_e_kernel(
                     start=True,
                     stop=True,
                 )
-                dst = g_rows[m][:, v0 : v0 + width]
-                nc.scalar.activation(dst, bank[:, :width], RELU)
+            nc.scalar.activation(g_rows[0][:, v0 : v0 + width], first_rows[:, :width], RELU)
+        nc.scalar.activation(g_rows[1][:], second_rows[:], RELU)
 
         parts = [[keep.tile([P, U], F32, name=f"parts{m}_{d}") for d in range(HOPS)] for m in range(N // P)]
         for m in range(N // P):

@@ -367,12 +367,14 @@ def tile_picked_hop2_relu_e_kernel(
                     stop=True,
                 )
             nc.scalar.activation(g_rows[0][:, v0 : v0 + width], first_rows[:, :width], RELU)
-        nc.scalar.activation(g_rows[1][:], second_rows[:], RELU)
+        nc.vector.tensor_scalar_max(g_rows[1][:], second_rows[:], 0.0)
 
-        parts = [[keep.tile([P, U], F32, name=f"parts{m}_{d}") for d in range(HOPS)] for m in range(N // P)]
+        parts = [[keep.tile([P, U], F32, name=f"parts{m}_{d}") for d in range(HOPS + 1)] for m in range(N // P)]
         for m in range(N // P):
-            for d in range(HOPS):
-                nc.vector.tensor_tensor(parts[m][d][:], g_rows[m][:].indirect(nxt_t[d][:]), gate2_t[d][:], MULT)
+            nc.scalar.activation(parts[m][2][:], g_rows[m][:].indirect(nxt_t[0][:]), COPY)
+            nc.vector.tensor_tensor(parts[m][1][:], g_rows[m][:].indirect(nxt_t[1][:]), gate2_t[1][:], MULT)
+        for m in range(N // P):
+            nc.vector.tensor_tensor(parts[m][0][:], parts[m][2][:], gate2_t[0][:], MULT)
         for m in range(N // P):
             result = keep.tile([P, U], F32, name=f"result{m}")
             nc.vector.tensor_tensor(result[:], parts[m][0][:], parts[m][1][:], ADD)

@@ -40,7 +40,7 @@ W_LOADS = [(0, 0, 256, "w_first"), (0, 256, 256, "w_raw0"), (1, 0, 384, "w_third
 
 TWO_STRETCHES = [(0, BANK), (BANK, BANK)]
 THREE_STRETCHES = [(0, BANK), (BANK, BANK // 2), (BANK + BANK // 2, BANK // 2)]
-WARM_UPS = 2
+WARM_UPS = (BANK, BANK // 2)
 HEAD = 3 * BANK // 2
 FOUR_STRETCHES = [(0, P), (P, 2 * P), (3 * P, 3 * P), (HEAD, S - HEAD)]
 STRETCHES = [FOUR_STRETCHES, TWO_STRETCHES, TWO_STRETCHES, TWO_STRETCHES]
@@ -49,6 +49,7 @@ LATE_BANKS = {(2, 0): 0, (2, 1): 1, (3, 0): 3, (3, 1): 4}
 
 Z_GROUPS = [(0, 2 * P), (2 * P, P), (3 * P, P)]
 TURNED_BLOCKS = 3
+FETCHED = (1, 2)
 G_BANKS = [1, 2, 7, 0]
 
 
@@ -184,13 +185,13 @@ def tile_picked_hop2_relu_e_kernel(
                 picked_scales[:, first : first + count], x_scales[:].indirect(entries(offs_t, first, count))
             )
         warm = psum.tile([P, BANK], F32, name="warm", tag="bank7")
-        for n in range(WARM_UPS):
+        for width in WARM_UPS:
             nc.tensor.matmul_mx(
-                out=warm[:],
+                out=warm[:, :width],
                 lhsT=picked0[:, :P].bitcast(FP8X4),
                 lhsT_scale=picked_scales[4:P, :P],
-                rhs=picked0[:, :BANK].bitcast(FP8X4),
-                rhs_scale=picked_scales[4:P, :BANK],
+                rhs=picked0[:, :width].bitcast(FP8X4),
+                rhs_scale=picked_scales[4:P, :width],
                 start=True,
                 stop=True,
             )
@@ -248,7 +249,18 @@ def tile_picked_hop2_relu_e_kernel(
             else:
                 nc.scalar.activation(dst, groups[(t, n)][:, :count], RELU)
 
+        fetched = {}
+
+        def fetch(t):
+            fetched[t] = keep.tile([P, wide], F32, name=f"fetched{t}", tag="w_early" if t == 2 else "fetched", align_bytes=ALIGN)
+            nc.scalar.activation(fetched[t][:], h_rows[t][:].indirect(entries(pos_t[0], 0, wide)), COPY)
+
         def weigh(t, d, v0, width):
+            if d == 0 and t in FETCHED and v0 < wide:
+                nc.vector.tensor_tensor(
+                    term(t, d, v0, width), fetched[t][:, v0 : v0 + width], gate_t[d][:, v0 : v0 + width], MULT
+                )
+                return
             nc.vector.tensor_tensor(
                 term(t, d, v0, width),
                 h_rows[t][:].indirect(entries(pos_t[d], v0, width)),
@@ -268,17 +280,20 @@ def tile_picked_hop2_relu_e_kernel(
             if t == 0:
                 keys = [(g, late_tile) for g in range(PASSES) for late_tile in (2, 3)]
                 quantise_w("late", late[:].rearrange("p g e m j -> p (g e m j)"), keys, tag="w_early")
-            for d in range(HOPS):
+            if t == 1:
+                fetch(t)
+            for d in (1, 0):
                 weigh(t, d, 0, V if t == 0 else wide)
         for t, n in LATE_BANKS:
             for g in range(PASSES):
                 multiply(t, g, n)
             leave_bank(t, n)
-        for d in range(HOPS):
-            weigh(2, d, 0, TURNED_BLOCKS * P)
+        fetch(2)
+        weigh(2, 1, 0, wide)
+        weigh(3, 0, 0, wide)
         for v0, width in Z_GROUPS[:2]:
-            for d in range(HOPS):
-                weigh(3, d, v0, width)
+            weigh(3, 1, v0, width)
+            weigh(2, 0, v0, width)
 
         first_sums = psum.tile([P, 2, 2, P], F32, name="first_sums", tag="bank1")
         sums = {(0, b): first_sums[:, b] for b in range(2)}
@@ -291,8 +306,8 @@ def tile_picked_hop2_relu_e_kernel(
                 sums[(t // 2, b)][:, t % 2, :],
                 lhsT=term(t, d, b * P, P),
                 rhs=identity[:],
-                start=(d == 0),
-                stop=(d == HOPS - 1),
+                start=(d == 0) != (t in FETCHED),
+                stop=(d == HOPS - 1) != (t in FETCHED),
                 is_transpose=True,
             )
 
@@ -308,15 +323,14 @@ def tile_picked_hop2_relu_e_kernel(
 
         for t in (0, 1):
             for b in range(TURNED_BLOCKS):
-                for d in range(HOPS):
+                for d in (1, 0) if t in FETCHED else (0, 1):
                     turn(t, b, d)
         for b in range(TURNED_BLOCKS):
             round_and_turn_back(0, b)
         for blocks in ((0, 1), (2,)):
-            for t in (2, 3):
-                for d in range(HOPS):
-                    for b in blocks:
-                        turn(t, b, d)
+            for t, d in ((3, 0), (3, 1), (2, 1), (2, 0)):
+                for b in blocks:
+                    turn(t, b, d)
             for b in blocks:
                 round_and_turn_back(1, b)
 
@@ -353,10 +367,12 @@ def tile_picked_hop2_relu_e_kernel(
 
         g_rows = [keep.tile([P, V], F32, name=f"g_rows{m}") for m in range(N // P)]
         second_rows = psum.tile([P, V], F32, name="second_rows", tag=f"bank{G_BANKS[-1]}")
+        second_last = psum.tile([P, P], F32, name="second_last", tag="bank4")
         for n, (v0, width) in enumerate(Z_GROUPS):
+            second_dst = second_rows[:, v0 : v0 + width] if v0 < wide else second_last[:]
             first_rows = psum.tile([P, BANK], F32, name=f"first_rows{n}", tag=f"bank{G_BANKS[n]}")
             z_words, z_scales = z_codes[n]
-            for m, dst in enumerate((first_rows[:, :width], second_rows[:, v0 : v0 + width])):
+            for m, dst in enumerate((first_rows[:, :width], second_dst)):
                 nc.tensor.matmul_mx(
                     out=dst,
                     lhsT=w2_codes[:, 2 * P * m : 2 * P * (m + 1)].bitcast(FP4X4),
@@ -367,7 +383,8 @@ def tile_picked_hop2_relu_e_kernel(
                     stop=True,
                 )
             nc.scalar.activation(g_rows[0][:, v0 : v0 + width], first_rows[:, :width], RELU)
-        nc.vector.tensor_scalar_max(g_rows[1][:], second_rows[:], 0.0)
+        nc.vector.tensor_scalar_max(g_rows[1][:, :wide], second_rows[:, :wide], 0.0)
+        nc.vector.tensor_scalar_max(g_rows[1][:, wide:], second_last[:], 0.0)
 
         parts = [[keep.tile([P, U], F32, name=f"parts{m}_{d}") for d in range(HOPS + 1)] for m in range(N // P)]
         for m in range(N // P):

@@ -40,7 +40,7 @@ W_LOADS = [(0, 0, 256, "w_first"), (0, 256, 256, "w_raw0"), (1, 0, 384, "w_third
 
 TWO_STRETCHES = [(0, BANK), (BANK, BANK)]
 THREE_STRETCHES = [(0, BANK), (BANK, BANK // 2), (BANK + BANK // 2, BANK // 2)]
-WARM_UPS = (BANK, BANK // 2)
+WARM_UPS = (BANK, BANK // 2, BANK // 4)
 HEAD = 3 * BANK // 2
 FOUR_STRETCHES = [(0, P), (P, 2 * P), (3 * P, 3 * P), (HEAD, S - HEAD)]
 STRETCHES = [FOUR_STRETCHES, TWO_STRETCHES, TWO_STRETCHES, TWO_STRETCHES]
@@ -209,6 +209,8 @@ def tile_picked_hop2_relu_e_kernel(
 
         def term(t, d, v0, width):
             first = (t - 1) % PACK * wide + v0 if v0 < wide else PACK * wide + t * P
+            if t == 3 and v0 < wide:
+                first = PACK * wide + P + v0
             return rows[d][:, first : first + width]
 
         h_rows = [keep.tile([P, S], F32, name=f"h{t}") for t in range(PACK)]
@@ -252,8 +254,9 @@ def tile_picked_hop2_relu_e_kernel(
         fetched = {}
 
         def fetch(t):
-            fetched[t] = keep.tile([P, wide], F32, name=f"fetched{t}", tag="w_early" if t == 2 else "fetched", align_bytes=ALIGN)
-            nc.scalar.activation(fetched[t][:], h_rows[t][:].indirect(entries(pos_t[0], 0, wide)), COPY)
+            tag = "w_early" if t == 2 else "fetched"
+            fetched[t] = keep.tile([P, wide], F32, name=f"fetched{t}", tag=tag, align_bytes=ALIGN)[:]
+            nc.scalar.activation(fetched[t], h_rows[t][:].indirect(entries(pos_t[0], 0, wide)), COPY)
 
         def weigh(t, d, v0, width):
             if d == 0 and t in FETCHED and v0 < wide:
@@ -295,11 +298,11 @@ def tile_picked_hop2_relu_e_kernel(
             weigh(3, 1, v0, width)
             weigh(2, 0, v0, width)
 
-        first_sums = psum.tile([P, 2, 2, P], F32, name="first_sums", tag="bank1")
+        first_sums = psum.tile([P, 2, 2, P], F32, name="first_sums", tag="bank4")
         sums = {(0, b): first_sums[:, b] for b in range(2)}
-        for (u, b), bank in {(0, 2): 0, (1, 0): 7, (1, 1): 2, (1, 2): 4}.items():
+        for (u, b), bank in {(0, 2): 3, (1, 0): 7, (1, 1): 2, (1, 2): 1}.items():
             sums[(u, b)] = psum.tile([P, 2, P], F32, name=f"sums{u}_{b}", tag=f"bank{bank}")[:]
-        back = [psum.tile([P, 2, P], F32, name=f"back{b}", tag=f"bank{bank}") for b, bank in enumerate((5, 6, 3))]
+        back = [psum.tile([P, 2, P], F32, name=f"back{b}", tag=f"bank{bank}") for b, bank in enumerate((5, 6, 0))]
 
         def turn(t, b, d):
             nc.tensor.matmul(
@@ -312,11 +315,7 @@ def tile_picked_hop2_relu_e_kernel(
             )
 
         def round_and_turn_back(u, b):
-            if u == 0 and b < HOPS:
-                first = PACK * wide + P + P // 2
-                words = rows[b][:, first : first + P]
-            else:
-                words = keep.tile([P, P], F32, name=f"turned{u}_{b}", align_bytes=ALIGN)[:]
+            words = keep.tile([P, P], F32, name=f"turned{u}_{b}", align_bytes=ALIGN)[:]
             pairs = words.bitcast(BF16).rearrange("v (m e) -> v m e", e=2)
             nc.scalar.copy(pairs, sums[(u, b)].rearrange("v e m -> v m e"))
             nc.tensor.transpose(back[b][:, u, :], words, identity[:])
@@ -334,8 +333,8 @@ def tile_picked_hop2_relu_e_kernel(
             for b in blocks:
                 round_and_turn_back(1, b)
 
-        for t in range(1, PACK):
-            for d in range(HOPS):
+        for d in range(HOPS):
+            for t in range(1, PACK):
                 weigh(t, d, wide, P)
 
         z01 = keep.tile([P, 2 * P, PACK], BF16, name="z01", align_bytes=ALIGN)
@@ -367,7 +366,7 @@ def tile_picked_hop2_relu_e_kernel(
 
         g_rows = [keep.tile([P, V], F32, name=f"g_rows{m}") for m in range(N // P)]
         second_rows = psum.tile([P, V], F32, name="second_rows", tag=f"bank{G_BANKS[-1]}")
-        second_last = psum.tile([P, P], F32, name="second_last", tag="bank4")
+        second_last = psum.tile([P, P], F32, name="second_last", tag="bank3")
         for n, (v0, width) in enumerate(Z_GROUPS):
             second_dst = second_rows[:, v0 : v0 + width] if v0 < wide else second_last[:]
             first_rows = psum.tile([P, BANK], F32, name=f"first_rows{n}", tag=f"bank{G_BANKS[n]}")

@@ -31,10 +31,10 @@ ALIGN = 64
 
 EVEN = 256
 QUICK = 160
-RELIEF = 448
+RELIEF = 416
 X_LOADS = [
     [(1024, 448), (512, EVEN), (512, QUICK)],
-    [(512, RELIEF), (512, 320), (256, 128), (256, 128), (256, 128), (128, 96), (128, 32)],
+    [(512, RELIEF), (512, 288), (256, 112), (256, 112), (256, 128), (128, 96), (128, 32)],
 ]
 W_LOADS = [(0, 0, 256, "w_first"), (0, 256, 256, "w_raw0"), (1, 0, 384, "w_third"), (1, 384, 128, "w_last")]
 
@@ -169,7 +169,7 @@ def tile_picked_hop2_relu_e_kernel(
         def quantise_w(name, source, keys, offset=None, tag=None):
             words = keep.tile([P, len(keys) * P], U32, name=f"w_words_{name}", tag=tag or name, align_bytes=ALIGN)
             if offset is None:
-                scales = keep.tile([P, len(keys) * P], U8, name=f"w_scales_{name}", align_bytes=ALIGN)
+                scales = keep.tile([P, len(keys) * P], U8, name=f"w_scales_{name}", tag=f"w_scales_{name}", align_bytes=ALIGN)
             else:
                 scales = shared.tile([P, len(keys) * P], U8, name=f"w_scales_{name}", offset=offset, align_bytes=ALIGN)
             nc.vector.quantize_mx(out=words[:].bitcast(FP8X4), scales=scales[:], in_=source)
@@ -298,11 +298,11 @@ def tile_picked_hop2_relu_e_kernel(
             weigh(3, 1, v0, width)
             weigh(2, 0, v0, width)
 
-        first_sums = psum.tile([P, 2, 2, P], F32, name="first_sums", tag="bank4")
+        first_sums = psum.tile([P, 2, 2, P], F32, name="first_sums", tag="bank1")
         sums = {(0, b): first_sums[:, b] for b in range(2)}
-        for (u, b), bank in {(0, 2): 3, (1, 0): 7, (1, 1): 2, (1, 2): 1}.items():
+        for (u, b), bank in {(0, 2): 0, (1, 0): 7, (1, 1): 2, (1, 2): 4}.items():
             sums[(u, b)] = psum.tile([P, 2, P], F32, name=f"sums{u}_{b}", tag=f"bank{bank}")[:]
-        back = [psum.tile([P, 2, P], F32, name=f"back{b}", tag=f"bank{bank}") for b, bank in enumerate((5, 6, 0))]
+        back = [psum.tile([P, 2, P], F32, name=f"back{b}", tag=f"bank{bank}") for b, bank in enumerate((5, 6, 3))]
 
         def turn(t, b, d):
             nc.tensor.matmul(
@@ -314,8 +314,13 @@ def tile_picked_hop2_relu_e_kernel(
                 is_transpose=True,
             )
 
+        low_words = keep.tile([P, wide], F32, name="low_words", tag="w_scales_late", align_bytes=ALIGN)
+
         def round_and_turn_back(u, b):
-            words = keep.tile([P, P], F32, name=f"turned{u}_{b}", align_bytes=ALIGN)[:]
+            if u == 0:
+                words = low_words[:, b * P : (b + 1) * P]
+            else:
+                words = keep.tile([P, P], F32, name=f"turned{b}", align_bytes=ALIGN)[:]
             pairs = words.bitcast(BF16).rearrange("v (m e) -> v m e", e=2)
             nc.scalar.copy(pairs, sums[(u, b)].rearrange("v e m -> v m e"))
             nc.tensor.transpose(back[b][:, u, :], words, identity[:])
@@ -366,7 +371,7 @@ def tile_picked_hop2_relu_e_kernel(
 
         g_rows = [keep.tile([P, V], F32, name=f"g_rows{m}") for m in range(N // P)]
         second_rows = psum.tile([P, V], F32, name="second_rows", tag=f"bank{G_BANKS[-1]}")
-        second_last = psum.tile([P, P], F32, name="second_last", tag="bank3")
+        second_last = psum.tile([P, P], F32, name="second_last", tag="bank4")
         for n, (v0, width) in enumerate(Z_GROUPS):
             second_dst = second_rows[:, v0 : v0 + width] if v0 < wide else second_last[:]
             first_rows = psum.tile([P, BANK], F32, name=f"first_rows{n}", tag=f"bank{G_BANKS[n]}")

@@ -309,8 +309,8 @@ def tile_picked_hop2_relu_e_kernel(
                 sums[(t // 2, b)][:, t % 2, :],
                 lhsT=term(t, d, b * P, P),
                 rhs=identity[:],
-                start=(d == 0) != (t in FETCHED),
-                stop=(d == HOPS - 1) != (t in FETCHED),
+                start=(t, d) in ((0, 0), (1, 1), (2, 1)),
+                stop=(t, d) in ((0, 1), (1, 0), (2, 0)),
                 is_transpose=True,
             )
 
@@ -332,7 +332,7 @@ def tile_picked_hop2_relu_e_kernel(
         for b in range(TURNED_BLOCKS):
             round_and_turn_back(0, b)
         for blocks in ((0, 1), (2,)):
-            for t, d in ((3, 0), (3, 1), (2, 1), (2, 0)):
+            for t, d in ((2, 1), (3, 0), (3, 1), (2, 0)):
                 for b in blocks:
                     turn(t, b, d)
             for b in blocks:

@@ -19,6 +19,7 @@ COPY = mybir.ActivationFunctionType.Copy
 RELU = mybir.ActivationFunctionType.Relu
 MULT = mybir.AluOpType.mult
 ADD = mybir.AluOpType.add
+IS_LT = mybir.AluOpType.is_lt
 
 P = 128
 PACK = 4
@@ -50,6 +51,11 @@ LATE_BANKS = {(2, 0): 0, (2, 1): 1, (3, 0): 3, (3, 1): 4}
 Z_GROUPS = [(0, 2 * P), (2 * P, P), (3 * P, P)]
 TURNED_BLOCKS = 3
 FETCHED = (1, 2)
+GATE_STEP = 5
+SECOND_GATE = 104
+TINY = 2.0**-60
+ROUNDED_AT = 4 * BANK
+ROUNDED_BYTES = 2 * PACK * (PASSES * T + PASSES * H)
 G_BANKS = [1, 2, 7, 0]
 
 
@@ -81,6 +87,10 @@ def tile_picked_hop2_relu_e_kernel(
         identity = keep.tile([P, P], F32, name="identity")
         make_identity(nc, identity[:])
 
+        gate_rows = keep.tile([P, P], F32, name="gate_rows")
+        pieces = gate.rearrange("d r (b v) -> (d r b) v", v=P)
+        nc.scalar.dma_start(gate_rows[:], pieces[: P * GATE_STEP : GATE_STEP])
+
         x_raw = []
         for g in range(PASSES):
             c0 = 0
@@ -99,12 +109,12 @@ def tile_picked_hop2_relu_e_kernel(
                 raw = keep.tile([P, PACK, width], F32, name=f"w_raw{g}_{c0}", tag=tag, align_bytes=ALIGN)
             nc.sync.dma_start(raw[:], pass_rows(w1, g)[:, :, c0 : c0 + width])
             w_raw.append((g, c0, width, raw))
-        pos_t, gate_t = [], []
-        for d, src in enumerate((pos1, pos2)):
-            pos_t.append(load_list(src, f"pos_t{d}"))
-            tile = keep.tile([P, V], F32, name=f"gate_t{d}")
-            nc.sync.dma_start(tile[:], gate[d])
-            gate_t.append(tile)
+        wide = TURNED_BLOCKS * P
+        pos_t = {d: load_list(src, f"pos_t{d}") for d, src in ((1, pos2), (0, pos1))}
+        second_weights = keep.tile([P, V], F32, name="second_weights")
+        nc.sync.dma_start(second_weights[:, wide:], gate[1][:, wide:])
+        first_weights = keep.tile([P, V - wide], F32, name="first_weights")
+        nc.sync.dma_start(first_weights[:], gate[0][:, wide:])
         w2_codes = keep.tile([P, 2 * N], U8, name="w2_codes", align_bytes=ALIGN)
         nc.sync.dma_start(w2_codes[:], w2_words[0])
         for q in range(4):
@@ -118,10 +128,35 @@ def tile_picked_hop2_relu_e_kernel(
             nc.sync.dma_start(tile[:], gate2[d])
             gate2_t.append(tile)
 
+        blocks = V // P
+        gate_cols = psum.tile([P, P], F32, name="gate_cols", tag="bank5")
+        nc.tensor.transpose(gate_cols[:], gate_rows[:], identity[:])
+        small = {
+            name: keep.tile([P, blocks], F32, name=name, align_bytes=ALIGN)
+            for name in ("square", "nudge", "lead", "inverse", "quotient")
+        }
+        room = shared.tile([P, ROUNDED_BYTES // 4], F32, name="room", offset=ROUNDED_AT, align_bytes=ALIGN)
+        both = room[:, : HOPS * blocks].rearrange("v (d b) -> v d b", d=HOPS)
+        by_four = gate_cols[:].rearrange("v (q b) -> v q b", b=blocks)
+        nc.scalar.activation(both, by_four[:, :: SECOND_GATE // blocks], COPY)
+        nc.vector.tensor_tensor(small["square"][:], both[:, 0], both[:, 0], MULT)
+        nc.vector.tensor_scalar(small["nudge"][:], small["square"][:], TINY * TINY, 2 * TINY, IS_LT, MULT)
+        nc.vector.tensor_tensor(small["lead"][:], both[:, 0], small["nudge"][:], ADD)
+        nc.vector.reciprocal(small["inverse"][:], small["lead"][:])
+        nc.vector.tensor_tensor(small["quotient"][:], small["inverse"][:], both[:, 1], MULT)
+        lead = small["lead"]
+        spread = psum.tile([P, wide], F32, name="spread", tag="bank6")
+        for b in range(TURNED_BLOCKS):
+            nc.tensor.transpose(
+                spread[:, b * P : (b + 1) * P], small["quotient"][:, b : b + 1].to_broadcast([P, P]), identity[:]
+            )
+        nc.scalar.copy(second_weights[:, :wide], spread[:])
+
         x_words = [keep.tile([P, T], U32, name=f"x_words{g}", align_bytes=ALIGN) for g in range(PASSES)]
         picked0 = keep.tile([P, S], U32, name="picked0", align_bytes=ALIGN)
         for n, (g, c0, width, share, raw) in enumerate(x_raw):
-            grouped = keep.tile([P, width, PACK], BF16, name=f"x_bf{n}", align_bytes=ALIGN)
+            at = ROUNDED_AT + 2 * PACK * (g * T + c0)
+            grouped = shared.tile([P, width, PACK], BF16, name=f"x_bf{n}", offset=at, align_bytes=ALIGN)
             dst = grouped[:].rearrange("p (c i) j -> p c j i", i=4)
             src = raw[:].rearrange("p j (c i) -> p c j i", i=4)
             if share > 0:
@@ -140,8 +175,9 @@ def tile_picked_hop2_relu_e_kernel(
             if (g, c0) == (1, 0):
                 nc.vector.tensor_copy(picked0[:], x_words[0][:].indirect(offs_t[:]))
 
-        early = keep.tile([P, 2, PASSES, P, PACK], BF16, name="w_early", tag="w_early", align_bytes=ALIGN)
-        late = keep.tile([P, PASSES, 2, P, PACK], BF16, name="w_late", align_bytes=ALIGN)
+        early_at = ROUNDED_AT + 2 * PACK * PASSES * T
+        early = shared.tile([P, 2, PASSES, P, PACK], BF16, name="w_early", offset=early_at, align_bytes=ALIGN)
+        late = shared.tile([P, PASSES, 2, P, PACK], BF16, name="w_late", offset=early_at + 2 * PACK * H, align_bytes=ALIGN)
 
         def deal(load, u, on_gpsimd, part=slice(None)):
             g, c0, width, raw = w_raw[load]
@@ -167,7 +203,10 @@ def tile_picked_hop2_relu_e_kernel(
         stationary = {}
 
         def quantise_w(name, source, keys, offset=None, tag=None):
-            words = keep.tile([P, len(keys) * P], U32, name=f"w_words_{name}", tag=tag or name, align_bytes=ALIGN)
+            if tag is None:
+                words = keep.tile([P, len(keys) * P], U32, name=f"w_words_{name}", align_bytes=ALIGN)
+            else:
+                words = shared.tile([P, len(keys) * P], U32, name=f"w_words_{name}", offset=early_at, align_bytes=ALIGN)
             if offset is None:
                 scales = keep.tile([P, len(keys) * P], U8, name=f"w_scales_{name}", tag=f"w_scales_{name}", align_bytes=ALIGN)
             else:
@@ -204,7 +243,6 @@ def tile_picked_hop2_relu_e_kernel(
         nc.vector.tensor_copy(tail[:], x_words[1][:].indirect(entries(offs_t, first, count)))
         quantise_w("second", early[:, 1].rearrange("p g m j -> p (g m j)"), [(0, 1), (1, 1)], 4 * count)
 
-        wide = TURNED_BLOCKS * P
         rows = [keep.tile([P, PACK * V], F32, name=f"terms{d}", align_bytes=ALIGN) for d in range(HOPS)]
 
         def term(t, d, v0, width):
@@ -254,22 +292,20 @@ def tile_picked_hop2_relu_e_kernel(
         fetched = {}
 
         def fetch(t):
-            tag = "w_early" if t == 2 else "fetched"
-            fetched[t] = keep.tile([P, wide], F32, name=f"fetched{t}", tag=tag, align_bytes=ALIGN)[:]
+            if t == 2:
+                fetched[t] = shared.tile([P, wide], F32, name="fetched2", offset=early_at, align_bytes=ALIGN)[:]
+            else:
+                fetched[t] = keep.tile([P, wide], F32, name="fetched1", align_bytes=ALIGN)[:]
             nc.scalar.activation(fetched[t], h_rows[t][:].indirect(entries(pos_t[0], 0, wide)), COPY)
 
         def weigh(t, d, v0, width):
-            if d == 0 and t in FETCHED and v0 < wide:
-                nc.vector.tensor_tensor(
-                    term(t, d, v0, width), fetched[t][:, v0 : v0 + width], gate_t[d][:, v0 : v0 + width], MULT
-                )
-                return
-            nc.vector.tensor_tensor(
-                term(t, d, v0, width),
-                h_rows[t][:].indirect(entries(pos_t[d], v0, width)),
-                gate_t[d][:, v0 : v0 + width],
-                MULT,
-            )
+            source = h_rows[t][:].indirect(entries(pos_t[d], v0, width))
+            if d == 1:
+                nc.vector.tensor_tensor(term(t, d, v0, width), source, second_weights[:, v0 : v0 + width], MULT)
+            elif v0 < wide:
+                nc.vector.tensor_copy(term(t, d, v0, width), source)
+            else:
+                nc.vector.tensor_tensor(term(t, d, v0, width), source, first_weights[:], MULT)
 
         for n in range(len(STRETCHES[0])):
             multiply(0, 0, n)
@@ -285,8 +321,10 @@ def tile_picked_hop2_relu_e_kernel(
                 quantise_w("late", late[:].rearrange("p g e m j -> p (g e m j)"), keys, tag="w_early")
             if t == 1:
                 fetch(t)
-            for d in (1, 0):
-                weigh(t, d, 0, V if t == 0 else wide)
+            weigh(t, 1, 0, V if t == 0 else wide)
+            if t == 0:
+                weigh(t, 0, 0, wide)
+                weigh(t, 0, wide, P)
         for t, n in LATE_BANKS:
             for g in range(PASSES):
                 multiply(t, g, n)
@@ -296,7 +334,6 @@ def tile_picked_hop2_relu_e_kernel(
         weigh(3, 0, 0, wide)
         for v0, width in Z_GROUPS[:2]:
             weigh(3, 1, v0, width)
-            weigh(2, 0, v0, width)
 
         first_sums = psum.tile([P, 2, 2, P], F32, name="first_sums", tag="bank1")
         sums = {(0, b): first_sums[:, b] for b in range(2)}
@@ -307,10 +344,10 @@ def tile_picked_hop2_relu_e_kernel(
         def turn(t, b, d):
             nc.tensor.matmul(
                 sums[(t // 2, b)][:, t % 2, :],
-                lhsT=term(t, d, b * P, P),
+                lhsT=fetched[t][:, b * P : (b + 1) * P] if d == 0 and t in FETCHED else term(t, d, b * P, P),
                 rhs=identity[:],
                 start=(t, d) in ((0, 0), (1, 1), (2, 1)),
-                stop=(t, d) in ((0, 1), (1, 0), (2, 0)),
+                stop=(t, d) in ((0, 1), (1, 0), (3, 1)),
                 is_transpose=True,
             )
 
@@ -322,7 +359,7 @@ def tile_picked_hop2_relu_e_kernel(
             else:
                 words = keep.tile([P, P], F32, name=f"turned{b}", align_bytes=ALIGN)[:]
             pairs = words.bitcast(BF16).rearrange("v (m e) -> v m e", e=2)
-            nc.scalar.copy(pairs, sums[(u, b)].rearrange("v e m -> v m e"))
+            nc.scalar.activation(pairs, sums[(u, b)].rearrange("v e m -> v m e"), COPY, scale=lead[:, b : b + 1])
             nc.tensor.transpose(back[b][:, u, :], words, identity[:])
 
         for t in (0, 1):
@@ -332,7 +369,7 @@ def tile_picked_hop2_relu_e_kernel(
         for b in range(TURNED_BLOCKS):
             round_and_turn_back(0, b)
         for blocks in ((0, 1), (2,)):
-            for t, d in ((2, 1), (3, 0), (3, 1), (2, 0)):
+            for t, d in ((2, 1), (3, 0), (2, 0), (3, 1)):
                 for b in blocks:
                     turn(t, b, d)
             for b in blocks:

import math
from contextlib import ExitStack

import concourse.mybir as mybir
from concourse.masks import make_identity

K, T, S, V, H, N, U = 1024, 2048, 1024, 512, 512, 256, 256
FLOPS = 2 * K * H * S + 2 * H * N * V

F32 = mybir.dt.float32
BF16 = mybir.dt.bfloat16
I32 = mybir.dt.int32
U32 = mybir.dt.uint32
U16 = mybir.dt.uint16
U8 = mybir.dt.uint8
FP8X4 = mybir.dt.float8_e4m3fn_x4
FP4X4 = mybir.dt.float4_e2m1fn_x4
COPY = mybir.ActivationFunctionType.Copy
RELU = mybir.ActivationFunctionType.Relu
MULT = mybir.AluOpType.mult
ADD = mybir.AluOpType.add
IS_LT = mybir.AluOpType.is_lt

P = 128
PACK = 4
K_PASS = P * PACK
PASSES = K // K_PASS
BANK = 512
STRIPE = 16
HOPS = 2
ALIGN = 64

EVEN = 256
QUICK = 160
RELIEF = 416
X_LOADS = [
    [(1024, 448), (512, EVEN), (512, QUICK)],
    [(512, RELIEF), (512, 288), (256, 112), (256, 112), (256, 128), (128, 96), (128, 32)],
]
W_LOADS = [(0, 0, 256, "w_first"), (0, 256, 256, "w_raw0"), (1, 0, 384, "w_third"), (1, 384, 128, "w_last")]

TWO_STRETCHES = [(0, BANK), (BANK, BANK)]
THREE_STRETCHES = [(0, BANK), (BANK, BANK // 2), (BANK + BANK // 2, BANK // 2)]
WARM_UPS = (BANK, BANK // 2, BANK // 4)
HEAD = 3 * BANK // 2
FOUR_STRETCHES = [(0, P), (P, 2 * P), (3 * P, 3 * P), (HEAD, S - HEAD)]
STRETCHES = [FOUR_STRETCHES, TWO_STRETCHES, TWO_STRETCHES, TWO_STRETCHES]
EARLY_BANKS = {(0, 0): 0, (0, 1): 1, (0, 2): 2, (0, 3): 5, (1, 0): 3, (1, 1): 4}
LATE_BANKS = {(2, 0): 0, (2, 1): 1, (3, 0): 3, (3, 1): 4}

Z_GROUPS = [(0, 2 * P), (2 * P, P), (3 * P, P)]
TURNED_BLOCKS = 3
FETCHED = (1, 2)
GATE_STEP = 5
SECOND_GATE = 104
TINY = 2.0**-60
ROUNDED_AT = 4 * BANK
ROUNDED_BYTES = 2 * PACK * (PASSES * T + PASSES * H)
G_BANKS = [1, 2, 7, 0]


def tile_picked_hop2_relu_e_kernel(
    tc, xT, w1, w2_words, w2_scales, gate, gate2, offs, pos1, pos2, nxt1, nxt2, out
):
    nc = tc.nc
    with ExitStack() as ctx:
        lists = ctx.enter_context(tc.tile_pool(name="lists", bufs=1))
        keep = ctx.enter_context(tc.tile_pool(name="keep", bufs=1))
        shared = ctx.enter_context(tc.tile_pool(name="shared", bufs=1))
        psum = ctx.enter_context(tc.psum_pool(name="psum", bufs=1))

        def load_list(src, name):
            tile = lists.tile(list(src.shape), U16, name=name)
            nc.sync.dma_start(tile[:], src)
            return tile

        def entries(list_tile, first, count):
            return list_tile[:, first // STRIPE : (first + count) // STRIPE]

        def pass_rows(matrix, g):
            return matrix[g * K_PASS : (g + 1) * K_PASS, :].rearrange("(p j) c -> p j c", j=PACK)

        x_scales = keep.tile([P, T], U8, name="x_scales", align_bytes=ALIGN)
        nc.gpsimd.memset(x_scales[:], 0)
        w2_plane = keep.tile([P, N], U8, name="w2_plane", align_bytes=ALIGN)
        nc.gpsimd.memset(w2_plane[:], 0)
        identity = keep.tile([P, P], F32, name="identity")
        make_identity(nc, identity[:])

        gate_rows = keep.tile([P, P], F32, name="gate_rows")
        pieces = gate.rearrange("d r (b v) -> (d r b) v", v=P)
        nc.scalar.dma_start(gate_rows[:], pieces[: P * GATE_STEP : GATE_STEP])

        x_raw = []
        for g in range(PASSES):
            c0 = 0
            for n, (width, share) in enumerate(X_LOADS[g]):
                raw = keep.tile([P, PACK, width], F32, name=f"x_raw{g}_{n}")
                nc.sync.dma_start(raw[:], pass_rows(xT, g)[:, :, c0 : c0 + width])
                x_raw.append((g, c0, width, share, raw))
                c0 += width
            if g == 0:
                offs_t = load_list(offs, "offs_t")
        w_raw = []
        for g, c0, width, tag in W_LOADS:
            if tag == "w_last":
                raw = shared.tile([P, PACK, width], F32, name="w_last", offset=0, align_bytes=ALIGN)
            else:
                raw = keep.tile([P, PACK, width], F32, name=f"w_raw{g}_{c0}", tag=tag, align_bytes=ALIGN)
            nc.sync.dma_start(raw[:], pass_rows(w1, g)[:, :, c0 : c0 + width])
            w_raw.append((g, c0, width, raw))
        wide = TURNED_BLOCKS * P
        pos_t = {d: load_list(src, f"pos_t{d}") for d, src in ((1, pos2), (0, pos1))}
        second_weights = keep.tile([P, V], F32, name="second_weights")
        nc.sync.dma_start(second_weights[:, wide:], gate[1][:, wide:])
        first_weights = keep.tile([P, V - wide], F32, name="first_weights")
        nc.sync.dma_start(first_weights[:], gate[0][:, wide:])
        w2_codes = keep.tile([P, 2 * N], U8, name="w2_codes", align_bytes=ALIGN)
        nc.sync.dma_start(w2_codes[:], w2_words[0])
        for q in range(4):
            nc.sync.dma_start(
                w2_plane[32 * q : 32 * q + 4, :].bitcast(I32), w2_scales[0, 4 * q : 4 * q + 4, :].bitcast(I32)
            )
        nxt_t, gate2_t = [], []
        for d, src in enumerate((nxt1, nxt2)):
            nxt_t.append(load_list(src, f"nxt_t{d}"))
            tile = keep.tile([P, U], F32, name=f"gate2_t{d}")
            nc.sync.dma_start(tile[:], gate2[d])
            gate2_t.append(tile)

        blocks = V // P
        gate_cols = psum.tile([P, P], F32, name="gate_cols", tag="bank5")
        nc.tensor.transpose(gate_cols[:], gate_rows[:], identity[:])
        small = {
            name: keep.tile([P, blocks], F32, name=name, align_bytes=ALIGN)
            for name in ("square", "nudge", "lead", "inverse", "quotient")
        }
        room = shared.tile([P, ROUNDED_BYTES // 4], F32, name="room", offset=ROUNDED_AT, align_bytes=ALIGN)
        both = room[:, : HOPS * blocks].rearrange("v (d b) -> v d b", d=HOPS)
        by_four = gate_cols[:].rearrange("v (q b) -> v q b", b=blocks)
        nc.scalar.activation(both, by_four[:, :: SECOND_GATE // blocks], COPY)
        nc.vector.tensor_tensor(small["square"][:], both[:, 0], both[:, 0], MULT)
        nc.vector.tensor_scalar(small["nudge"][:], small["square"][:], TINY * TINY, 2 * TINY, IS_LT, MULT)
        nc.vector.tensor_tensor(small["lead"][:], both[:, 0], small["nudge"][:], ADD)
        nc.vector.reciprocal(small["inverse"][:], small["lead"][:])
        nc.vector.tensor_tensor(small["quotient"][:], small["inverse"][:], both[:, 1], MULT)
        lead = small["lead"]
        spread = psum.tile([P, wide], F32, name="spread", tag="bank6")
        for b in range(TURNED_BLOCKS):
            nc.tensor.transpose(
                spread[:, b * P : (b + 1) * P], small["quotient"][:, b : b + 1].to_broadcast([P, P]), identity[:]
            )
        nc.scalar.copy(second_weights[:, :wide], spread[:])

        x_words = [keep.tile([P, T], U32, name=f"x_words{g}", align_bytes=ALIGN) for g in range(PASSES)]
        picked0 = keep.tile([P, S], U32, name="picked0", align_bytes=ALIGN)
        for n, (g, c0, width, share, raw) in enumerate(x_raw):
            at = ROUNDED_AT + 2 * PACK * (g * T + c0)
            grouped = shared.tile([P, width, PACK], BF16, name=f"x_bf{n}", offset=at, align_bytes=ALIGN)
            dst = grouped[:].rearrange("p (c i) j -> p c j i", i=4)
            src = raw[:].rearrange("p j (c i) -> p c j i", i=4)
            if share > 0:
                nc.scalar.activation(dst[:, : share // 4], src[:, : share // 4], COPY)
            if share < width:
                nc.vector.tensor_copy(dst[:, share // 4 :], src[:, share // 4 :])
            q0 = 0
            while q0 < width:
                count = min(BANK, 2 ** int(math.log2(width - q0)))
                nc.vector.quantize_mx(
                    out=x_words[g][:, c0 + q0 : c0 + q0 + count].bitcast(FP8X4),
                    scales=x_scales[4 - 4 * g : P, c0 + q0 : c0 + q0 + count],
                    in_=grouped[:, q0 : q0 + count].rearrange("p c j -> p (c j)"),
                )
                q0 += count
            if (g, c0) == (1, 0):
                nc.vector.tensor_copy(picked0[:], x_words[0][:].indirect(offs_t[:]))

        early_at = ROUNDED_AT + 2 * PACK * PASSES * T
        early = shared.tile([P, 2, PASSES, P, PACK], BF16, name="w_early", offset=early_at, align_bytes=ALIGN)
        late = shared.tile([P, PASSES, 2, P, PACK], BF16, name="w_late", offset=early_at + 2 * PACK * H, align_bytes=ALIGN)

        def deal(load, u, on_gpsimd, part=slice(None)):
            g, c0, width, raw = w_raw[load]
            tile = early[:, :, g] if u == 0 else late[:, g]
            dst = tile.rearrange("p e m j -> p m j e")[:, c0 // PACK : (c0 + width) // PACK]
            src = raw[:].rearrange("p j (m t) -> p m j t", t=PACK)[:, :, :, 2 * u : 2 * u + 2]
            dst, src = dst[:, part], src[:, part]
            if on_gpsimd:
                order = "p m j e -> p m e j"
                nc.gpsimd.tensor_scalar(dst.rearrange(order), src.rearrange(order), 1.0, 0.0, MULT, ADD)
            else:
                nc.scalar.copy(dst, src)

        for load in (0, 1):
            deal(load, 0, False)
            deal(load, 1, True)
        deal(2, 0, False, slice(0, 80))
        deal(2, 0, True, slice(80, 96))
        deal(3, 0, False)
        deal(3, 1, True)
        deal(2, 1, False)

        stationary = {}

        def quantise_w(name, source, keys, offset=None, tag=None):
            if tag is None:
                words = keep.tile([P, len(keys) * P], U32, name=f"w_words_{name}", align_bytes=ALIGN)
            else:
                words = shared.tile([P, len(keys) * P], U32, name=f"w_words_{name}", offset=early_at, align_bytes=ALIGN)
            if offset is None:
                scales = keep.tile([P, len(keys) * P], U8, name=f"w_scales_{name}", tag=f"w_scales_{name}", align_bytes=ALIGN)
            else:
                scales = shared.tile([P, len(keys) * P], U8, name=f"w_scales_{name}", offset=offset, align_bytes=ALIGN)
            nc.vector.quantize_mx(out=words[:].bitcast(FP8X4), scales=scales[:], in_=source)
            for n, key in enumerate(keys):
                stationary[key] = (words[:, n * P : (n + 1) * P], scales[:, n * P : (n + 1) * P])

        def quantise_early(g):
            quantise_w(f"early{g}", early[:, 0, g].rearrange("p m j -> p (m j)"), [(g, 0)])

        picked_scales = keep.tile([P, S], U8, name="picked_scales", align_bytes=ALIGN)
        for first, count in TWO_STRETCHES:
            nc.vector.tensor_copy(
                picked_scales[:, first : first + count], x_scales[:].indirect(entries(offs_t, first, count))
            )
        warm = psum.tile([P, BANK], F32, name="warm", tag="bank7")
        for width in WARM_UPS:
            nc.tensor.matmul_mx(
                out=warm[:, :width],
                lhsT=picked0[:, :P].bitcast(FP8X4),
                lhsT_scale=picked_scales[4:P, :P],
                rhs=picked0[:, :width].bitcast(FP8X4),
                rhs_scale=picked_scales[4:P, :width],
                start=True,
                stop=True,
            )
        quantise_early(0)
        head = keep.tile([P, HEAD], U32, name="picked1_head", tag="w_raw0", align_bytes=ALIGN)
        nc.vector.tensor_copy(head[:], x_words[1][:].indirect(entries(offs_t, 0, HEAD)))
        quantise_early(1)
        first, count = THREE_STRETCHES[2]
        tail = shared.tile([P, count], U32, name="picked1_tail", offset=0, align_bytes=ALIGN)
        nc.vector.tensor_copy(tail[:], x_words[1][:].indirect(entries(offs_t, first, count)))
        quantise_w("second", early[:, 1].rearrange("p g m j -> p (g m j)"), [(0, 1), (1, 1)], 4 * count)

        rows = [keep.tile([P, PACK * V], F32, name=f"terms{d}", align_bytes=ALIGN) for d in range(HOPS)]

        def term(t, d, v0, width):
            first = (t - 1) % PACK * wide + v0 if v0 < wide else PACK * wide + t * P
            if t == 3 and v0 < wide:
                first = PACK * wide + P + v0
            return rows[d][:, first : first + width]

        h_rows = [keep.tile([P, S], F32, name=f"h{t}") for t in range(PACK)]
        bank_of = EARLY_BANKS | LATE_BANKS
        groups = {}

        def multiply(t, g, n):
            first, count = STRETCHES[t][n]
            if g == 0:
                groups[(t, n)] = psum.tile([P, BANK], F32, name=f"h_bank{t}_{n}", tag=f"bank{bank_of[(t, n)]}")
                pieces = [(first, count, picked0[:, first : first + count])]
                if count == 3 * P:
                    pieces = [(f, c, picked0[:, f : f + c]) for f, c in ((first, 2 * P), (first + 2 * P, P))]
            else:
                in_head = min(count, HEAD - first)
                pieces = [(first, in_head, head[:, first : first + in_head])] if in_head > 0 else []
                if count == 3 * P:
                    pieces = [(f, c, head[:, f : f + c]) for f, c in ((first, 2 * P), (first + 2 * P, P))]
                if first + count > HEAD:
                    pieces.append((HEAD, S - HEAD, tail[:]))
            words, scales = stationary[(g, t)]
            for f, c, moving in pieces:
                nc.tensor.matmul_mx(
                    out=groups[(t, n)][:, f - first : f - first + c],
                    lhsT=words.bitcast(FP8X4),
                    lhsT_scale=scales,
                    rhs=moving.bitcast(FP8X4),
                    rhs_scale=picked_scales[4 - 4 * g : P, f : f + c],
                    start=(g == 0 and f == first),
                    stop=(g == PASSES - 1 and f + c == first + count),
                )

        def leave_bank(t, n):
            first, count = STRETCHES[t][n]
            dst = h_rows[t][:, first : first + count]
            if (t, n) == (0, 0):
                nc.vector.tensor_scalar_max(dst, groups[(t, n)][:, :count], 0.0)
            else:
                nc.scalar.activation(dst, groups[(t, n)][:, :count], RELU)

        fetched = {}

        def fetch(t):
            if t == 2:
                fetched[t] = shared.tile([P, wide], F32, name="fetched2", offset=early_at, align_bytes=ALIGN)[:]
            else:
                fetched[t] = keep.tile([P, wide], F32, name="fetched1", align_bytes=ALIGN)[:]
            nc.scalar.activation(fetched[t], h_rows[t][:].indirect(entries(pos_t[0], 0, wide)), COPY)

        def weigh(t, d, v0, width):
            source = h_rows[t][:].indirect(entries(pos_t[d], v0, width))
            if d == 1:
                nc.vector.tensor_tensor(term(t, d, v0, width), source, second_weights[:, v0 : v0 + width], MULT)
            elif v0 < wide:
                nc.vector.tensor_copy(term(t, d, v0, width), source)
            else:
                nc.vector.tensor_tensor(term(t, d, v0, width), source, first_weights[:], MULT)

        for n in range(len(STRETCHES[0])):
            multiply(0, 0, n)
        for t in (0, 1):
            for n in range(len(STRETCHES[t])):
                if t == 1:
                    multiply(t, 0, n)
                multiply(t, 1, n)
            for n in range(len(STRETCHES[t])):
                leave_bank(t, n)
            if t == 0:
                keys = [(g, late_tile) for g in range(PASSES) for late_tile in (2, 3)]
                quantise_w("late", late[:].rearrange("p g e m j -> p (g e m j)"), keys, tag="w_early")
            if t == 1:
                fetch(t)
            weigh(t, 1, 0, V if t == 0 else wide)
            if t == 0:
                weigh(t, 0, 0, wide)
                weigh(t, 0, wide, P)
        for t, n in LATE_BANKS:
            for g in range(PASSES):
                multiply(t, g, n)
            leave_bank(t, n)
        fetch(2)
        weigh(2, 1, 0, wide)
        weigh(3, 0, 0, wide)
        for v0, width in Z_GROUPS[:2]:
            weigh(3, 1, v0, width)

        first_sums = psum.tile([P, 2, 2, P], F32, name="first_sums", tag="bank1")
        sums = {(0, b): first_sums[:, b] for b in range(2)}
        for (u, b), bank in {(0, 2): 0, (1, 0): 7, (1, 1): 2, (1, 2): 4}.items():
            sums[(u, b)] = psum.tile([P, 2, P], F32, name=f"sums{u}_{b}", tag=f"bank{bank}")[:]
        back = [psum.tile([P, 2, P], F32, name=f"back{b}", tag=f"bank{bank}") for b, bank in enumerate((5, 6, 3))]

        def turn(t, b, d):
            nc.tensor.matmul(
                sums[(t // 2, b)][:, t % 2, :],
                lhsT=fetched[t][:, b * P : (b + 1) * P] if d == 0 and t in FETCHED else term(t, d, b * P, P),
                rhs=identity[:],
                start=(t, d) in ((0, 0), (1, 1), (2, 1)),
                stop=(t, d) in ((0, 1), (1, 0), (3, 1)),
                is_transpose=True,
            )

        low_words = keep.tile([P, wide], F32, name="low_words", tag="w_scales_late", align_bytes=ALIGN)

        def round_and_turn_back(u, b):
            if u == 0:
                words = low_words[:, b * P : (b + 1) * P]
            else:
                words = keep.tile([P, P], F32, name=f"turned{b}", align_bytes=ALIGN)[:]
            pairs = words.bitcast(BF16).rearrange("v (m e) -> v m e", e=2)
            nc.scalar.activation(pairs, sums[(u, b)].rearrange("v e m -> v m e"), COPY, scale=lead[:, b : b + 1])
            nc.tensor.transpose(back[b][:, u, :], words, identity[:])

        for t in (0, 1):
            for b in range(TURNED_BLOCKS):
                for d in (1, 0) if t in FETCHED else (0, 1):
                    turn(t, b, d)
        for b in range(TURNED_BLOCKS):
            round_and_turn_back(0, b)
        for blocks in ((0, 1), (2,)):
            for t, d in ((2, 1), (3, 0), (2, 0), (3, 1)):
                for b in blocks:
                    turn(t, b, d)
            for b in blocks:
                round_and_turn_back(1, b)

        for d in range(HOPS):
            for t in range(1, PACK):
                weigh(t, d, wide, P)

        z01 = keep.tile([P, 2 * P, PACK], BF16, name="z01", align_bytes=ALIGN)
        z2 = keep.tile([P, P, PACK], BF16, name="z2", align_bytes=ALIGN)
        for b, block in enumerate((z01[:, :P], z01[:, P:], z2[:])):
            pairs = block.rearrange("p v t -> p (v t)").bitcast(F32).rearrange("p (v u) -> p v u", u=2)
            nc.scalar.copy(pairs, back[b][:].rearrange("p u v -> p v u"))

        z_codes = []
        for n, (v0, width) in enumerate(Z_GROUPS):
            z_words = keep.tile([P, width], U32, name=f"z_words{n}", align_bytes=ALIGN)
            z_scales = keep.tile([P, width], U8, name=f"z_scales{n}", align_bytes=ALIGN)
            z_codes.append((z_words, z_scales))

        def quantise_z(n, c0, source):
            z_words, z_scales = z_codes[n]
            nc.vector.quantize_mx(
                out=z_words[:, c0 : c0 + P].bitcast(FP8X4),
                scales=z_scales[:, c0 : c0 + P],
                in_=source.rearrange("p v t -> p (v t)"),
            )

        quantise_z(0, 0, z01[:, :P])
        quantise_z(0, P, z01[:, P:])
        views = [rows[d][:, PACK * wide :].rearrange("p (t c i) -> p c t i", t=PACK, i=2) for d in range(HOPS)]
        nc.vector.tensor_tensor(z01[:, :P].rearrange("p (c i) t -> p c t i", i=2), views[0], views[1], ADD)
        quantise_z(1, 0, z2[:])
        quantise_z(2, 0, z01[:, :P])

        g_rows = [keep.tile([P, V], F32, name=f"g_rows{m}") for m in range(N // P)]
        second_rows = psum.tile([P, V], F32, name="second_rows", tag=f"bank{G_BANKS[-1]}")
        second_last = psum.tile([P, P], F32, name="second_last", tag="bank4")
        for n, (v0, width) in enumerate(Z_GROUPS):
            second_dst = second_rows[:, v0 : v0 + width] if v0 < wide else second_last[:]
            first_rows = psum.tile([P, BANK], F32, name=f"first_rows{n}", tag=f"bank{G_BANKS[n]}")
            z_words, z_scales = z_codes[n]
            for m, dst in enumerate((first_rows[:, :width], second_dst)):
                nc.tensor.matmul_mx(
                    out=dst,
                    lhsT=w2_codes[:, 2 * P * m : 2 * P * (m + 1)].bitcast(FP4X4),
                    lhsT_scale=w2_plane[:, P * m : P * (m + 1)],
                    rhs=z_words[:].bitcast(FP8X4),
                    rhs_scale=z_scales[:],
                    start=True,
                    stop=True,
                )
            nc.scalar.activation(g_rows[0][:, v0 : v0 + width], first_rows[:, :width], RELU)
        nc.vector.tensor_scalar_max(g_rows[1][:, :wide], second_rows[:, :wide], 0.0)
        nc.vector.tensor_scalar_max(g_rows[1][:, wide:], second_last[:], 0.0)

        parts = [[keep.tile([P, U], F32, name=f"parts{m}_{d}") for d in range(HOPS + 1)] for m in range(N // P)]
        for m in range(N // P):
            nc.scalar.activation(parts[m][2][:], g_rows[m][:].indirect(nxt_t[0][:]), COPY)
            nc.vector.tensor_tensor(parts[m][1][:], g_rows[m][:].indirect(nxt_t[1][:]), gate2_t[1][:], MULT)
        for m in range(N // P):
            nc.vector.tensor_tensor(parts[m][0][:], parts[m][2][:], gate2_t[0][:], MULT)
        for m in range(N // P):
            result = keep.tile([P, U], F32, name=f"result{m}")
            nc.vector.tensor_tensor(result[:], parts[m][0][:], parts[m][1][:], ADD)
            nc.sync.dma_start(out[m * P : (m + 1) * P, :], result[:])
